import numpy as np
import ml_dtypes


def mxq(x, axis, fmt="e4m3"):
    dtype, down = {"e4m3": (ml_dtypes.float8_e4m3fn, 7), "e5m2": (ml_dtypes.float8_e5m2, 14)}[fmt]
    v = np.moveaxis(np.asarray(x, np.float32).astype(ml_dtypes.bfloat16).astype(np.float64), axis, -1)
    blocks = v.reshape(v.shape[:-1] + (-1, 32))
    amax = np.abs(blocks).max(-1, keepdims=True)
    byte = np.maximum(np.where(amax > 0, np.frexp(amax)[1] - 1 + 127, 0) - down, 1)
    scale = np.exp2(byte - 127.0)
    codes = (blocks / scale).astype(np.float32).astype(dtype).astype(np.float64)
    return np.moveaxis((codes * scale).reshape(v.shape), -1, axis)


WIDE = False


def mx_kscale(k):
    if not WIDE:
        return np.ones(k)
    levels = np.array([10, -10, 5, -5, 0])
    if k % 512:
        return np.exp2(np.random.permutation(np.resize(levels, k // 32))).repeat(32)
    a = np.empty((k // 512, 16))
    for p in range(k // 512):
        a[p, :8] = np.random.permutation(np.resize(levels, 8))
        for g in range(8):
            far = levels[np.abs(levels - a[p, g]) >= 10]
            a[p, g + 8] = far[np.random.randint(len(far))]
    return np.exp2(a.ravel()).repeat(32)


def f64(x):
    return np.asarray(x).astype(np.float64)


def striped(idx):
    return np.tile(idx.reshape(-1, 16).T, (8, 1)).astype(np.uint16)


def unstriped(offs):
    return offs[:16].T.reshape(-1).astype(np.int64)


E2M1 = np.array([0.0, 0.5, 1.0, 1.5, 2.0, 3.0, 4.0, 6.0, -0.0, -0.5, -1.0, -1.5, -2.0, -3.0, -4.0, -6.0])


def pack_weight(w, fmt):
    k, n = w.shape
    w = f64(np.asarray(w, np.float32).astype(ml_dtypes.bfloat16)).reshape(k // 32, 32, n)
    amax = np.abs(w).max(1)
    if fmt == "e4m3":
        byte = np.frexp(amax)[1] - 1 + 127 - 7
    else:
        mant, ex = np.frexp(amax / 6.0)
        byte = np.where(mant > 0.5, ex, ex - 1) + 127
    byte = np.clip(np.where(amax > 0, byte, 1), 1, 254)
    scaled = (w * np.exp2(127.0 - byte)[:, None, :]).reshape(k, n).astype(np.float32)
    by_word = np.ascontiguousarray(scaled.reshape(k // 512, 128, 4, n).transpose(0, 1, 3, 2))
    if fmt == "e4m3":
        words = by_word.astype(ml_dtypes.float8_e4m3fn).view(np.uint8)
    else:
        c = by_word.astype(ml_dtypes.float4_e2m1fn).view(np.uint8) & 0xF
        words = (c[..., 0::2] | (c[..., 1::2] << 4)).reshape(k // 512, 128, 2 * n)
    return np.ascontiguousarray(words), np.ascontiguousarray(byte.astype(np.uint8).reshape(k // 512, 16, n))


def unpack_weight(words, scales, fmt):
    g, _, n = scales.shape
    words = np.ascontiguousarray(words).reshape(g, 128, n, -1)
    if fmt == "e4m3":
        vals = words.view(ml_dtypes.float8_e4m3fn).astype(np.float64)
    else:
        nib = np.empty((g, 128, n, 4), np.uint8)
        nib[..., 0::2] = words & 0xF
        nib[..., 1::2] = words >> 4
        vals = E2M1[nib]
    vals = vals * np.repeat(np.exp2(scales.astype(np.float64) - 127.0), 8, axis=1)[..., None]
    return vals.transpose(0, 1, 3, 2).reshape(g * 512, n)


def gelu(v):
    return 0.5 * v * (1.0 + np.tanh(np.sqrt(2.0 / np.pi) * (v + 0.044715 * v**3)))


def bf(x):
    return np.asarray(x, np.float32).astype(ml_dtypes.bfloat16)

def planes(Y):
    n, m = Y.shape
    b = f64(bf(Y)).reshape(n // 32, 32, m)
    amax = np.abs(b).max(1)
    byte = np.clip(np.where(amax > 0, np.frexp(amax)[1] - 1 + 127 - 7, 1), 1, 254)
    codes = (b * np.exp2(127.0 - byte)[:, None, :]).reshape(n, m).astype(np.float32).astype(ml_dtypes.float8_e4m3fn).view(np.uint8)
    words = codes.reshape(n // 512, 128, 4, m).transpose(0, 1, 3, 2)
    return np.ascontiguousarray(words), np.ascontiguousarray(byte.astype(np.uint8).reshape(n // 512, 16, m))


K, T, S, H, N = 1024, 4096, 1024, 512, 1024

def setup_inputs():
    n = np.random.standard_normal
    s = mx_kscale(K)[:, None]
    u = mx_kscale(H)[:, None]
    c = 1 / np.sqrt(K)
    tab_words, tab_scales = pack_weight(n((K, T)) * s, "e4m3")
    wi_words, wi_scales = pack_weight(0.5 * c * n((K, H)) / s, "e4m3")
    wc_words, wc_scales = pack_weight(0.6 * c * n((K, H)) / s, "e2m1")
    wp_words, wp_scales = pack_weight(0.8 * c * n((K, H)) / s * u.T, "e2m1")
    return {
        "tab_words": tab_words, "tab_scales": tab_scales,
        "offs": striped(np.random.permutation(T)[:S]),
        "offs2": striped(np.random.permutation(T)[:S]),
        "offs3": striped(np.random.permutation(T)[:S]),
        "ws": (c * n((K, H)) / s * u.T).astype(np.float32),
        "wi_words": wi_words, "wi_scales": wi_scales,
        "wc_words": wc_words, "wc_scales": wc_scales,
        "wp_words": wp_words, "wp_scales": wp_scales,
        "wd": (n((H, N)) / np.sqrt(H) / u).astype(np.float32),
        "gain": (0.7 * np.exp(0.8 * n(N))).astype(np.float32),
    }

def reference(tab_words, tab_scales, offs, offs2, offs3, ws, wi_words, wi_scales,
              wc_words, wc_scales, wp_words, wp_scales, wd, gain):
    v = unpack_weight(tab_words, tab_scales, "e4m3")
    vs, vc, vp = v[:, unstriped(offs)], v[:, unstriped(offs2)], v[:, unstriped(offs3)]
    wi = unpack_weight(wi_words, wi_scales, "e4m3")
    wc = unpack_weight(wc_words, wc_scales, "e2m1")
    wp = unpack_weight(wp_words, wp_scales, "e2m1")
    a = mxq(f64(ws), 0, "e4m3").T @ vs
    crowd = wi.T @ vs + wc.T @ vc
    pred = wp.T @ vp
    h = a * (1.0 - crowd) - pred
    y = f64(gain)[:, None] * (mxq(f64(wd), 0, "e4m3").T @ mxq(h, 0, "e4m3"))
    words, scales = planes(y)
    return y, words, scales

@@ -1,0 +1,326 @@
+from contextlib import ExitStack
+
+import concourse.mybir as mybir
+from concourse.masks import make_identity
+
+K, T, S, H, N = 1024, 4096, 1024, 512, 1024
+FLOPS = 2 * (4 * K * H * S + H * N * S)
+
+F32 = mybir.dt.float32
+BF16 = mybir.dt.bfloat16
+I32 = mybir.dt.int32
+U32 = mybir.dt.uint32
+U16 = mybir.dt.uint16
+U8 = mybir.dt.uint8
+FP8X4 = mybir.dt.float8_e4m3fn_x4
+FP4X4 = mybir.dt.float4_e2m1fn_x4
+COPY = mybir.ActivationFunctionType.Copy
+MULT = mybir.AluOpType.mult
+ADD = mybir.AluOpType.add
+SUBTRACT = mybir.AluOpType.subtract
+
+P = 128
+PASSES = 2
+HALF = 512
+BLOCK = 128
+QUARTER = 256
+GROUPS = 2
+
+
+def tile_list_competition_dispersal_kernel(
+    tc, tab_words, tab_scales, offs, offs2, offs3, ws, wi_words, wi_scales,
+    wc_words, wc_scales, wp_words, wp_scales, wd, gain, out_0, out_1, out_2,
+):
+    nc = tc.nc
+    with ExitStack() as ctx:
+        keep = ctx.enter_context(tc.tile_pool(name="keep", bufs=1))
+        ring = ctx.enter_context(tc.tile_pool(name="ring", bufs=2))
+        psum = ctx.enter_context(tc.psum_pool(name="psum", bufs=8))
+
+        tab_plane = keep.tile([P, T], U8, name="tab_plane", align_bytes=64)
+        nc.vector.memset(tab_plane[:, 0:2816].bitcast(I32), 0)
+        nc.gpsimd.memset(tab_plane[:, 2816:T].bitcast(I32), 0)
+        lists = []
+        for n, src in enumerate((offs, offs2, offs3)):
+            lst = keep.tile([P, S // 16], U16, name="list%d" % n)
+            lists.append(lst)
+        for n in (2, 1, 0):
+            nc.sync.dma_start(lists[n][:], (offs, offs2, offs3)[n])
+        for q in range(4):
+            nc.sync.dma_start(
+                out=tab_plane[32 * q : 32 * q + 8, :].bitcast(I32),
+                in_=tab_scales[:, 4 * q : 4 * q + 4, :].bitcast(I32),
+            )
+        tab = []
+
+        def load_table(a):
+            words = keep.tile([P, T], I32, name="tab%d" % a, align_bytes=64)
+            nc.sync.dma_start(out=words[:], in_=tab_words[a].rearrange("p t i -> p (t i)").bitcast(I32))
+            tab.append(words)
+
+        load_table(0)
+        w_planes = keep.tile([P, 3, PASSES, H], U8, name="w_planes", align_bytes=64)
+        nc.gpsimd.memset(w_planes[:].rearrange("p w a c -> p (w a c)").bitcast(I32), 0)
+        for w, src in enumerate((wi_scales, wc_scales, wp_scales)):
+            nc.sync.dma_start(
+                out=w_planes[0:16, w, :, :].bitcast(I32),
+                in_=src.rearrange("a q c -> q a c").bitcast(I32),
+            )
+        load_table(1)
+        wc = keep.tile([P, PASSES, 2 * H], U8, name="wc", align_bytes=64)
+        nc.sync.dma_start(out=wc[:].bitcast(I32), in_=wc_words.rearrange("a p c -> p a c").bitcast(I32))
+        wi = []
+
+        def load_wi(a):
+            words = keep.tile([P, H], I32, name="wi%d" % a, align_bytes=64)
+            nc.sync.dma_start(out=words[:], in_=wi_words[a].rearrange("p c i -> p (c i)").bitcast(I32))
+            wi.append(words)
+
+        load_wi(0)
+        ws_raw, wd_raw = [], []
+
+        def load_ws(a):
+            raw = keep.tile([P, 4, H], F32, name="ws_raw%d" % a)
+            nc.sync.dma_start(out=raw[:], in_=ws[512 * a : 512 * (a + 1), :].rearrange("(p i) c -> p i c", i=4))
+            ws_raw.append(raw)
+
+        def load_wd(g):
+            raw = keep.tile([P, 4, 512], F32, name="wd_raw%d" % g)
+            nc.sync.dma_start(out=raw[:], in_=wd[:, 512 * g : 512 * (g + 1)].rearrange("(p i) n -> p i n", i=4))
+            wd_raw.append(raw)
+
+        load_ws(0)
+
+        fp4_planes = keep.tile([P, 2, S], U8, name="fp4_planes", align_bytes=64)
+        nc.vector.tensor_copy(fp4_planes[:, 1, :], tab_plane[:].indirect(lists[2][:]))
+        nc.vector.tensor_copy(fp4_planes[:, 0, :], tab_plane[:].indirect(lists[1][:]))
+        own_planes = keep.tile([P, S], U8, name="own_planes", align_bytes=64)
+        nc.vector.tensor_copy(own_planes[:], tab_plane[:].indirect(lists[0][:]))
+        lifted = keep.tile([P, 2, S], U8, name="lifted", align_bytes=64)
+        nc.gpsimd.memset(lifted[:].rearrange("p l s -> p (l s)").bitcast(I32), 0)
+        nc.sync.dma_start(
+            out=lifted[0:100].rearrange("p l s -> p (l s)").bitcast(I32),
+            in_=fp4_planes[4:104].rearrange("p l s -> p (l s)").bitcast(I32),
+        )
+        load_wi(1)
+        gains = keep.tile([P, GROUPS, 4], F32, name="gains")
+        nc.sync.dma_start(out=gains[:], in_=gain.rearrange("(g p t) -> p g t", g=GROUPS, t=4))
+        flat_planes = w_planes[:].rearrange("p w a c -> p (w a c)").bitcast(I32)
+        for q in range(1, 4):
+            nc.sync.dma_start(out=flat_planes[32 * q : 32 * q + 4, :], in_=flat_planes[4 * q : 4 * q + 4, :])
+
+        load_ws(1)
+        load_wd(0)
+        wp = keep.tile([P, PASSES, 2 * H], U8, name="wp", align_bytes=64)
+        nc.sync.dma_start(out=wp[:].bitcast(I32), in_=wp_words.rearrange("a p c -> p a c").bitcast(I32))
+        load_wd(1)
+
+        ident = keep.tile([P, P], F32, name="ident")
+        make_identity(nc, ident[:])
+
+        picked = {}
+
+        def gather_words(lst, a, half, tag):
+            words = keep.tile([P, HALF], U32, name="picked_%d_%d_%d" % (lst, a, half), tag=tag, align_bytes=64)
+            cols = slice(half * HALF // 16, (half + 1) * HALF // 16)
+            nc.vector.tensor_copy(words[:], tab[a][:].bitcast(U32).indirect(lists[lst][:, cols]))
+            picked[lst, a, half] = words
+
+        ws_codes = keep.tile([P, PASSES, H], U32, name="ws_codes", align_bytes=64)
+        ws_planes = keep.tile([P, PASSES, H], U8, align_bytes=64)
+
+        def quantise_ws(a):
+            grouped = keep.tile([P, H, 4], BF16, name="ws_bf%d" % a, tag="ws_bf%d" % a, align_bytes=64)
+            nc.scalar.copy(out=grouped[:], in_=ws_raw[a][:].rearrange("p i c -> p c i"))
+            nc.vector.quantize_mx(
+                out=ws_codes[:, a, :].bitcast(FP8X4), scales=ws_planes[:, a, :],
+                in_=grouped[:].rearrange("p c i -> p (c i)"),
+            )
+
+        wd_codes = keep.tile([P, GROUPS, 512], U32, name="wd_codes", align_bytes=64)
+        wd_planes = keep.tile([P, GROUPS, 512], U8, align_bytes=64)
+
+        def quantise_wd(g, copy):
+            grouped = keep.tile([P, 4, P, 4], BF16, name="wd_bf%d" % g, align_bytes=64)
+            copy(out=grouped[:].rearrange("p t m i -> p m t i"),
+                 in_=wd_raw[g][:].rearrange("p i (m t) -> p m t i", t=4))
+            nc.vector.quantize_mx(
+                out=wd_codes[:, g, :].bitcast(FP8X4), scales=wd_planes[:, g, :],
+                in_=grouped[:].rearrange("p t m i -> p (t m i)"),
+            )
+
+        def stationary(lst, a, blk):
+            half, c0 = divmod(blk * BLOCK, HALF)
+            cols = slice(blk * BLOCK, (blk + 1) * BLOCK)
+            words = picked[lst, a, half][:, c0 : c0 + BLOCK].bitcast(FP8X4)
+            if lst == 0:
+                plane = own_planes[4 * a : P, cols]
+            elif a == 0:
+                plane = fp4_planes[:, lst - 1, cols]
+            else:
+                plane = lifted[:, lst - 1, cols]
+            return words, plane
+
+        def product(bank, terms, blk, start=True, stop=True):
+            for n, (lst, a, words, plane) in enumerate(terms):
+                lhs, lhs_plane = stationary(lst, a, blk)
+                nc.tensor.matmul_mx(out=bank[:], lhsT=lhs, lhsT_scale=lhs_plane, rhs=words, rhs_scale=plane,
+                                    start=(start and n == 0), stop=(stop and n == len(terms) - 1))
+
+        def dealt(ap):
+            return ap.rearrange("j (p u e) -> j u p e", u=2, e=2)
+
+        def pairs(ap):
+            return ap.rearrange("j (u p e) -> j u p e", u=2, e=2)
+
+        room = {}
+
+        c_banks = {}
+
+        def crowding(blk, a):
+            if a == 0:
+                c_banks[blk] = psum.tile([P, H], F32, name="crowd_bank", tag="bank")
+            terms = [(1, a, wc[:, a, :].bitcast(FP4X4), w_planes[:, 1, a, :]),
+                     (0, a, wi[a][:].bitcast(FP8X4), w_planes[:, 0, a, :])]
+            product(c_banks[blk], terms, blk, start=(a == 0), stop=(a == 1))
+            if a == 1:
+                u = keep.tile([P, H], F32, name="room%d" % blk)
+                nc.scalar.activation(out=pairs(u[:]), in_=dealt(c_banks[blk][:]), func=COPY, scale=-1.0, bias=1.0)
+                room[blk] = u
+
+        h_quant, h_rows = {}, {}
+
+        a_banks, p_banks = {}, {}
+
+        def abundance(blk):
+            a_banks[blk] = psum.tile([P, H], F32, name="a_bank", tag="bank")
+            product(a_banks[blk], [(0, a, ws_codes[:, a, :].bitcast(FP8X4), ws_planes[:, a, :]) for a in range(PASSES)], blk)
+
+        def predation(blk):
+            p_banks[blk] = psum.tile([P, H], F32, name="p_bank", tag="bank")
+            product(p_banks[blk], [(2, a, wp[:, a, :].bitcast(FP4X4), w_planes[:, 2, a, :]) for a in range(PASSES)], blk)
+
+        def growth(quarter):
+            blks = (2 * quarter, 2 * quarter + 1)
+            grown, hs = {}, {}
+            for blk in blks:
+                grown[blk] = ring.tile([P, H], F32, name="grown", tag="grown")
+                nc.vector.tensor_tensor(pairs(grown[blk][:]), dealt(a_banks[blk][:]), pairs(room[blk][:]), MULT)
+            for blk in blks:
+                hs[blk] = ring.tile([P, H], BF16, name="h_rows", tag="h_rows", bufs=4, align_bytes=64)
+                nc.vector.tensor_tensor(pairs(hs[blk][:]), pairs(grown[blk][:]), dealt(p_banks[blk][:]), SUBTRACT)
+            h_rows[quarter] = hs
+
+        def turn(quarter):
+            blks = (2 * quarter, 2 * quarter + 1)
+            hs = h_rows[quarter]
+            turned = psum.tile([P, 2, 2, BLOCK], F32, name="turned", tag="bank")
+            for b, blk in enumerate(blks):
+                words = hs[blk][:].bitcast(F32)
+                for u in range(2):
+                    nc.tensor.transpose(turned[:, b, u, :], words[:, u * P : (u + 1) * P], ident[:])
+            grouped = ring.tile([P, QUARTER * 4], BF16, name="h_grouped", tag="h_grouped", align_bytes=64)
+            nc.scalar.copy(out=grouped[:].bitcast(F32).rearrange("p (b j u) -> p b j u", b=2, u=2),
+                           in_=turned[:].rearrange("p b u j -> p b j u"))
+            h_quant[quarter] = grouped
+
+        early_planes = keep.tile([P, GROUPS, HALF], U8, name="early_planes", align_bytes=64)
+        last_planes = keep.tile([P, GROUPS, HALF], U8, name="last_planes", align_bytes=64)
+
+        h_codes = {}
+
+        def quantise_h(quarter):
+            codes = ring.tile([P, QUARTER], U32, name="h_codes", tag="h_codes", bufs=4, align_bytes=64)
+            plane = ring.tile([P, QUARTER], U8, name="h_plane", tag="h_plane", bufs=4, align_bytes=64)
+            nc.vector.quantize_mx(out=codes[:].bitcast(FP8X4), scales=plane[:], in_=h_quant[quarter][:])
+            h_codes[quarter] = (codes, plane)
+
+        def disperse(quarter, g, cast, on_vector):
+            cols = slice(quarter * QUARTER, (quarter + 1) * QUARTER)
+            codes, plane = h_codes[quarter]
+            y = ring.tile([P, 4, QUARTER], F32, name="y", tag="y", bufs=8)
+            for pair in range(2):
+                bank = psum.tile([P, 2, QUARTER], F32, name="y_bank", tag="bank")
+                for e in range(2):
+                    t = 2 * pair + e
+                    nc.tensor.matmul_mx(
+                        out=bank[:, e, :],
+                        lhsT=wd_codes[:, g, t * P : (t + 1) * P].bitcast(FP8X4),
+                        lhsT_scale=wd_planes[:, g, t * P : (t + 1) * P],
+                        rhs=codes[:].bitcast(FP8X4), rhs_scale=plane[:], start=True, stop=True,
+                    )
+                for e in range(2):
+                    t = 2 * pair + e
+                    if pair in on_vector:
+                        nc.vector.tensor_scalar(y[:, t, :], bank[:, e, :], gains[:, g, t : t + 1], None, MULT)
+                    else:
+                        nc.scalar.activation(out=y[:, t, :], in_=bank[:, e, :], func=COPY, scale=gains[:, g, t : t + 1])
+            nc.sync.dma_start(
+                out=out_0[512 * g : 512 * (g + 1), cols].rearrange("(p t) j -> p t j", t=4), in_=y[:])
+            grouped = ring.tile([P, QUARTER, 4], BF16, name="y_grouped", tag="y_grouped", bufs=4, align_bytes=64)
+            cast(out=grouped[:], in_=y[:].rearrange("p t j -> p j t"))
+            y_codes = ring.tile([P, QUARTER], U32, name="y_codes", tag="y_codes", bufs=8, align_bytes=64)
+            nc.vector.quantize_mx(out=y_codes[:].bitcast(FP8X4), scales=(early_planes if quarter < 2 else last_planes)[:, g, (quarter % 2) * QUARTER : (quarter % 2 + 1) * QUARTER],
+                                  in_=grouped[:].rearrange("p j t -> p (j t)"))
+            nc.sync.dma_start(
+                out=out_1[g, :, cols, :].rearrange("p m t -> p (m t)").bitcast(I32), in_=y_codes[:].bitcast(I32))
+
+        def store_scales(planes, cols):
+            for q in range(4):
+                nc.sync.dma_start(
+                    out=out_2[:, 4 * q : 4 * q + 4, cols].rearrange("g r m -> r g m").bitcast(I32),
+                    in_=planes[32 * q : 32 * q + 4, :, :].bitcast(I32),
+                )
+
+        on_s, on_v = nc.scalar.copy, nc.vector.tensor_copy
+
+        def on_g(out, in_):
+            nc.gpsimd.tensor_scalar(out, in_, 1.0, 0.0, MULT, ADD)
+
+        for half in range(2):
+            for lst in (1, 0):
+                gather_words(lst, 0, half, "w%d0%d" % (lst, half))
+        for half in range(2):
+            gather_words(2, 0, half, "w20%d" % half)
+        for half in range(2):
+            for lst in (1, 0):
+                gather_words(lst, 1, half, "w%d1%d" % (lst, half))
+        for a in range(PASSES):
+            quantise_ws(a)
+            gather_words(2, 1, a, "ws_bf%d" % a)
+        quantise_wd(0, on_s)
+        for a in range(PASSES):
+            for blk in range(8):
+                crowding(blk, a)
+        for blk in range(4):
+            abundance(blk)
+            predation(blk)
+        growth(0)
+        turn(0)
+        quantise_h(0)
+        for blk in (4, 5):
+            abundance(blk)
+            predation(blk)
+        disperse(0, 0, on_s, ())
+        quantise_wd(1, on_s)
+        growth(1)
+        turn(1)
+        quantise_h(1)
+        disperse(0, 1, on_v, ())
+        for blk in (6, 7):
+            abundance(blk)
+            predation(blk)
+        growth(2)
+        disperse(1, 0, on_v, ())
+        turn(2)
+        quantise_h(2)
+        growth(3)
+        disperse(1, 1, on_v, ())
+        turn(3)
+        quantise_h(3)
+        store_scales(early_planes, slice(0, HALF))
+        disperse(2, 0, on_v, ())
+        disperse(2, 1, on_v, ())
+        disperse(3, 0, on_v, ())
+        disperse(3, 1, on_v, ())
+        store_scales(last_planes, slice(HALF, S))

@@ -25,6 +25,7 @@ HALF = 512
 BLOCK = 128
 QUARTER = 256
 GROUPS = 2
+EARLY = 3 * QUARTER
 
 
 def tile_list_competition_dispersal_kernel(
@@ -89,7 +90,7 @@ def tile_list_competition_dispersal_kernel(
             nc.sync.dma_start(out=raw[:], in_=wd[:, 512 * g : 512 * (g + 1)].rearrange("(p i) n -> p i n", i=4))
             wd_raw.append(raw)
 
-        load_ws(0)
+        load_wi(1)
 
         fp4_planes = keep.tile([P, 2, S], U8, name="fp4_planes", align_bytes=64)
         nc.vector.tensor_copy(fp4_planes[:, 1, :], tab_plane[:].indirect(lists[2][:]))
@@ -99,20 +100,20 @@ def tile_list_competition_dispersal_kernel(
         lifted = keep.tile([P, 2, S], U8, name="lifted", align_bytes=64)
         nc.gpsimd.memset(lifted[:].rearrange("p l s -> p (l s)").bitcast(I32), 0)
         nc.sync.dma_start(
-            out=lifted[0:100].rearrange("p l s -> p (l s)").bitcast(I32),
-            in_=fp4_planes[4:104].rearrange("p l s -> p (l s)").bitcast(I32),
+            out=lifted[0:112].rearrange("p l s -> p (l s)").bitcast(I32),
+            in_=fp4_planes[4:116].rearrange("p l s -> p (l s)").bitcast(I32),
         )
-        load_wi(1)
         gains = keep.tile([P, GROUPS, 4], F32, name="gains")
         nc.sync.dma_start(out=gains[:], in_=gain.rearrange("(g p t) -> p g t", g=GROUPS, t=4))
+        wp = keep.tile([P, PASSES, 2 * H], U8, name="wp", align_bytes=64)
+        nc.sync.dma_start(out=wp[:].bitcast(I32), in_=wp_words.rearrange("a p c -> p a c").bitcast(I32))
         flat_planes = w_planes[:].rearrange("p w a c -> p (w a c)").bitcast(I32)
         for q in range(1, 4):
             nc.sync.dma_start(out=flat_planes[32 * q : 32 * q + 4, :], in_=flat_planes[4 * q : 4 * q + 4, :])
 
+        load_ws(0)
         load_ws(1)
         load_wd(0)
-        wp = keep.tile([P, PASSES, 2 * H], U8, name="wp", align_bytes=64)
-        nc.sync.dma_start(out=wp[:].bitcast(I32), in_=wp_words.rearrange("a p c -> p a c").bitcast(I32))
         load_wd(1)
 
         ident = keep.tile([P, P], F32, name="ident")
@@ -177,14 +178,14 @@ def tile_list_competition_dispersal_kernel(
 
         c_banks = {}
 
-        def crowding(blk, a):
-            if a == 0:
+        def crowding(blk, a, first):
+            if first:
                 c_banks[blk] = psum.tile([P, H], F32, name="crowd_bank", tag="bank")
             terms = [(1, a, wc[:, a, :].bitcast(FP4X4), w_planes[:, 1, a, :]),
                      (0, a, wi[a][:].bitcast(FP8X4), w_planes[:, 0, a, :])]
-            product(c_banks[blk], terms, blk, start=(a == 0), stop=(a == 1))
-            if a == 1:
-                u = keep.tile([P, H], F32, name="room%d" % blk)
+            product(c_banks[blk], terms, blk, start=first, stop=not first)
+            if not first:
+                u = keep.tile([P, H], F32, name="room%d" % blk, tag="room%d" % blk, align_bytes=64)
                 nc.scalar.activation(out=pairs(u[:]), in_=dealt(c_banks[blk][:]), func=COPY, scale=-1.0, bias=1.0)
                 room[blk] = u
 
@@ -206,9 +207,10 @@ def tile_list_competition_dispersal_kernel(
             for blk in blks:
                 grown[blk] = ring.tile([P, H], F32, name="grown", tag="grown")
                 nc.vector.tensor_tensor(pairs(grown[blk][:]), dealt(a_banks[blk][:]), pairs(room[blk][:]), MULT)
+            both = keep.tile([P, 2, H], BF16, name="h_rows", tag="h%d" % quarter, align_bytes=64)
             for blk in blks:
-                hs[blk] = ring.tile([P, H], BF16, name="h_rows", tag="h_rows", bufs=4, align_bytes=64)
-                nc.vector.tensor_tensor(pairs(hs[blk][:]), pairs(grown[blk][:]), dealt(p_banks[blk][:]), SUBTRACT)
+                hs[blk] = both[:, blk % 2, :]
+                nc.vector.tensor_tensor(pairs(hs[blk]), pairs(grown[blk][:]), dealt(p_banks[blk][:]), SUBTRACT)
             h_rows[quarter] = hs
 
         def turn(quarter):
@@ -216,17 +218,15 @@ def tile_list_competition_dispersal_kernel(
             hs = h_rows[quarter]
             turned = psum.tile([P, 2, 2, BLOCK], F32, name="turned", tag="bank")
             for b, blk in enumerate(blks):
-                words = hs[blk][:].bitcast(F32)
+                words = hs[blk].bitcast(F32)
                 for u in range(2):
                     nc.tensor.transpose(turned[:, b, u, :], words[:, u * P : (u + 1) * P], ident[:])
-            grouped = ring.tile([P, QUARTER * 4], BF16, name="h_grouped", tag="h_grouped", align_bytes=64)
+            grouped = keep.tile([P, QUARTER * 4], BF16, name="h_grouped", tag="h%d" % (quarter + 1), align_bytes=64)
             nc.scalar.copy(out=grouped[:].bitcast(F32).rearrange("p (b j u) -> p b j u", b=2, u=2),
                            in_=turned[:].rearrange("p b u j -> p b j u"))
             h_quant[quarter] = grouped
 
-        early_planes = keep.tile([P, GROUPS, HALF], U8, name="early_planes", align_bytes=64)
-        last_planes = keep.tile([P, GROUPS, HALF], U8, name="last_planes", align_bytes=64)
-
+        y_planes = keep.tile([P, GROUPS, S], U8, name="y_planes", align_bytes=64)
         h_codes = {}
 
         def quantise_h(quarter):
@@ -235,7 +235,7 @@ def tile_list_competition_dispersal_kernel(
             nc.vector.quantize_mx(out=codes[:].bitcast(FP8X4), scales=plane[:], in_=h_quant[quarter][:])
             h_codes[quarter] = (codes, plane)
 
-        def disperse(quarter, g, cast, on_vector):
+        def disperse(quarter, g, on_vector):
             cols = slice(quarter * QUARTER, (quarter + 1) * QUARTER)
             codes, plane = h_codes[quarter]
             y = ring.tile([P, 4, QUARTER], F32, name="y", tag="y", bufs=8)
@@ -249,27 +249,42 @@ def tile_list_competition_dispersal_kernel(
                         lhsT_scale=wd_planes[:, g, t * P : (t + 1) * P],
                         rhs=codes[:].bitcast(FP8X4), rhs_scale=plane[:], start=True, stop=True,
                     )
-                for e in range(2):
-                    t = 2 * pair + e
-                    if pair in on_vector:
-                        nc.vector.tensor_scalar(y[:, t, :], bank[:, e, :], gains[:, g, t : t + 1], None, MULT)
-                    else:
+                if pair in on_vector:
+                    ts = slice(2 * pair, 2 * pair + 2)
+                    nc.vector.tensor_tensor(
+                        y[:, ts, :], bank[:], gains[:, g, ts].unsqueeze(2).to_broadcast([P, 2, QUARTER]), MULT)
+                else:
+                    for e in range(2):
+                        t = 2 * pair + e
                         nc.scalar.activation(out=y[:, t, :], in_=bank[:, e, :], func=COPY, scale=gains[:, g, t : t + 1])
             nc.sync.dma_start(
                 out=out_0[512 * g : 512 * (g + 1), cols].rearrange("(p t) j -> p t j", t=4), in_=y[:])
-            grouped = ring.tile([P, QUARTER, 4], BF16, name="y_grouped", tag="y_grouped", bufs=4, align_bytes=64)
-            cast(out=grouped[:], in_=y[:].rearrange("p t j -> p j t"))
-            y_codes = ring.tile([P, QUARTER], U32, name="y_codes", tag="y_codes", bufs=8, align_bytes=64)
-            nc.vector.quantize_mx(out=y_codes[:].bitcast(FP8X4), scales=(early_planes if quarter < 2 else last_planes)[:, g, (quarter % 2) * QUARTER : (quarter % 2 + 1) * QUARTER],
-                                  in_=grouped[:].rearrange("p j t -> p (j t)"))
-            nc.sync.dma_start(
-                out=out_1[g, :, cols, :].rearrange("p m t -> p (m t)").bitcast(I32), in_=y_codes[:].bitcast(I32))
+            ys[quarter, g] = y
 
-        def store_scales(planes, cols):
+        ys, y_bf = {}, {}
+        y_codes = [keep.tile([P, GROUPS, QUARTER], U32, name="y_codes%d" % q, align_bytes=64) for q in range(4)]
+
+        def regroup(quarter, g, cast):
+            y = ys[quarter, g]
+            grouped = ring.tile([P, QUARTER, 4], BF16, name="y_grouped", tag="y_grouped", bufs=8, align_bytes=64)
+            cast(out=grouped[:], in_=y[:].rearrange("p t j -> p j t"))
+            y_bf[quarter, g] = grouped
+
+        def quantise_y(quarter, g):
+            cols = slice(quarter * QUARTER, (quarter + 1) * QUARTER)
+            nc.vector.quantize_mx(out=y_codes[quarter][:, g, :].bitcast(FP8X4), scales=y_planes[:, g, cols],
+                                  in_=y_bf[quarter, g][:].rearrange("p j t -> p (j t)"))
+
+        def store_codes(quarter):
+            cols = slice(quarter * QUARTER, (quarter + 1) * QUARTER)
+            nc.sync.dma_start(
+                out=out_1[:, :, cols, :].rearrange("g p m t -> p g (m t)").bitcast(I32), in_=y_codes[quarter][:].bitcast(I32))
+
+        def store_scales():
             for q in range(4):
                 nc.sync.dma_start(
-                    out=out_2[:, 4 * q : 4 * q + 4, cols].rearrange("g r m -> r g m").bitcast(I32),
-                    in_=planes[32 * q : 32 * q + 4, :, :].bitcast(I32),
+                    out=out_2[:, 4 * q : 4 * q + 4, :].rearrange("g r m -> r g m").bitcast(I32),
+                    in_=y_planes[32 * q : 32 * q + 4, :, :].bitcast(I32),
                 )
 
         on_s, on_v = nc.scalar.copy, nc.vector.tensor_copy
@@ -277,50 +292,59 @@ def tile_list_competition_dispersal_kernel(
         def on_g(out, in_):
             nc.gpsimd.tensor_scalar(out, in_, 1.0, 0.0, MULT, ADD)
 
+        casts = (on_g, on_g, on_g, on_g, on_g, on_g, on_s, on_v)
+
         for half in range(2):
             for lst in (1, 0):
                 gather_words(lst, 0, half, "w%d0%d" % (lst, half))
-        for half in range(2):
-            gather_words(2, 0, half, "w20%d" % half)
+        gather_words(2, 0, 0, "w200")
         for half in range(2):
             for lst in (1, 0):
                 gather_words(lst, 1, half, "w%d1%d" % (lst, half))
-        for a in range(PASSES):
-            quantise_ws(a)
-            gather_words(2, 1, a, "ws_bf%d" % a)
-        quantise_wd(0, on_s)
+        quantise_ws(0)
+        gather_words(2, 1, 0, "ws_bf0")
+        quantise_ws(1)
+        gather_words(2, 0, 1, "ws_bf1")
         for a in range(PASSES):
             for blk in range(8):
-                crowding(blk, a)
+                crowding(blk, a, a == 0)
         for blk in range(4):
             abundance(blk)
             predation(blk)
         growth(0)
         turn(0)
+        quantise_wd(0, on_g)
         quantise_h(0)
+        quantise_wd(1, on_g)
         for blk in (4, 5):
             abundance(blk)
-            predation(blk)
-        disperse(0, 0, on_s, ())
-        quantise_wd(1, on_s)
+        disperse(0, 0, ())
         growth(1)
+        gather_words(2, 1, 1, "room3")
+        disperse(0, 1, ())
         turn(1)
         quantise_h(1)
-        disperse(0, 1, on_v, ())
+        for blk in (4, 5):
+            predation(blk)
         for blk in (6, 7):
             abundance(blk)
             predation(blk)
         growth(2)
-        disperse(1, 0, on_v, ())
+        disperse(1, 0, ())
         turn(2)
         quantise_h(2)
+        disperse(1, 1, ())
         growth(3)
-        disperse(1, 1, on_v, ())
+        disperse(2, 0, ())
         turn(3)
         quantise_h(3)
-        store_scales(early_planes, slice(0, HALF))
-        disperse(2, 0, on_v, ())
-        disperse(2, 1, on_v, ())
-        disperse(3, 0, on_v, ())
-        disperse(3, 1, on_v, ())
-        store_scales(last_planes, slice(HALF, S))
+        disperse(2, 1, ())
+        disperse(3, 0, ())
+        disperse(3, 1, (0, 1))
+        for quarter in range(4):
+            for g in range(GROUPS):
+                regroup(quarter, g, casts[2 * quarter + g])
+            for g in range(GROUPS):
+                quantise_y(quarter, g)
+            store_codes(quarter)
+        store_scales()

@@ -45,12 +45,12 @@ def tile_list_competition_dispersal_kernel(
         for n, src in enumerate((offs, offs2, offs3)):
             lst = keep.tile([P, S // 16], U16, name="list%d" % n)
             lists.append(lst)
-        for n in (2, 1, 0):
+        for n in range(3):
             nc.sync.dma_start(lists[n][:], (offs, offs2, offs3)[n])
-        for q in range(4):
+        for r in range(4):
             nc.sync.dma_start(
-                out=tab_plane[32 * q : 32 * q + 8, :].bitcast(I32),
-                in_=tab_scales[:, 4 * q : 4 * q + 4, :].bitcast(I32),
+                out=tab_plane[r:P:16, :].bitcast(I32),
+                in_=tab_scales.rearrange("a (q r) t -> r q a t", r=4)[r].bitcast(I32),
             )
         tab = []
 
@@ -90,30 +90,28 @@ def tile_list_competition_dispersal_kernel(
             nc.sync.dma_start(out=raw[:], in_=wd[:, 512 * g : 512 * (g + 1)].rearrange("(p i) n -> p i n", i=4))
             wd_raw.append(raw)
 
-        load_wi(1)
+        load_ws(0)
 
-        fp4_planes = keep.tile([P, 2, S], U8, name="fp4_planes", align_bytes=64)
-        nc.vector.tensor_copy(fp4_planes[:, 1, :], tab_plane[:].indirect(lists[2][:]))
-        nc.vector.tensor_copy(fp4_planes[:, 0, :], tab_plane[:].indirect(lists[1][:]))
-        own_planes = keep.tile([P, S], U8, name="own_planes", align_bytes=64)
-        nc.vector.tensor_copy(own_planes[:], tab_plane[:].indirect(lists[0][:]))
-        lifted = keep.tile([P, 2, S], U8, name="lifted", align_bytes=64)
+        planes = keep.tile([P, 3, S], U8, name="planes", align_bytes=64)
+        for lst in range(3):
+            nc.vector.tensor_copy(planes[:, lst, :], tab_plane[:].indirect(lists[lst][:]))
+        lifted = keep.tile([P, 3, S], U8, name="lifted", align_bytes=64)
         nc.gpsimd.memset(lifted[:].rearrange("p l s -> p (l s)").bitcast(I32), 0)
         nc.sync.dma_start(
             out=lifted[0:112].rearrange("p l s -> p (l s)").bitcast(I32),
-            in_=fp4_planes[4:116].rearrange("p l s -> p (l s)").bitcast(I32),
+            in_=planes[16:128].rearrange("p l s -> p (l s)").bitcast(I32),
         )
+        load_wi(1)
         gains = keep.tile([P, GROUPS, 4], F32, name="gains")
         nc.sync.dma_start(out=gains[:], in_=gain.rearrange("(g p t) -> p g t", g=GROUPS, t=4))
-        wp = keep.tile([P, PASSES, 2 * H], U8, name="wp", align_bytes=64)
-        nc.sync.dma_start(out=wp[:].bitcast(I32), in_=wp_words.rearrange("a p c -> p a c").bitcast(I32))
         flat_planes = w_planes[:].rearrange("p w a c -> p (w a c)").bitcast(I32)
         for q in range(1, 4):
             nc.sync.dma_start(out=flat_planes[32 * q : 32 * q + 4, :], in_=flat_planes[4 * q : 4 * q + 4, :])
 
-        load_ws(0)
         load_ws(1)
         load_wd(0)
+        wp = keep.tile([P, PASSES, 2 * H], U8, name="wp", align_bytes=64)
+        nc.sync.dma_start(out=wp[:].bitcast(I32), in_=wp_words.rearrange("a p c -> p a c").bitcast(I32))
         load_wd(1)
 
         ident = keep.tile([P, P], F32, name="ident")
@@ -132,7 +130,8 @@ def tile_list_competition_dispersal_kernel(
 
         def quantise_ws(a):
             grouped = keep.tile([P, H, 4], BF16, name="ws_bf%d" % a, tag="ws_bf%d" % a, align_bytes=64)
-            nc.scalar.copy(out=grouped[:], in_=ws_raw[a][:].rearrange("p i c -> p c i"))
+            nc.scalar.copy(out=grouped[:].rearrange("p (c n) i -> p c i n", n=4),
+                           in_=ws_raw[a][:].rearrange("p i (c n) -> p c i n", n=4))
             nc.vector.quantize_mx(
                 out=ws_codes[:, a, :].bitcast(FP8X4), scales=ws_planes[:, a, :],
                 in_=grouped[:].rearrange("p c i -> p (c i)"),
@@ -141,12 +140,13 @@ def tile_list_competition_dispersal_kernel(
         wd_codes = keep.tile([P, GROUPS, 512], U32, name="wd_codes", align_bytes=64)
         wd_planes = keep.tile([P, GROUPS, 512], U8, align_bytes=64)
 
-        def quantise_wd(g, copy):
-            grouped = keep.tile([P, 4, P, 4], BF16, name="wd_bf%d" % g, align_bytes=64)
-            copy(out=grouped[:].rearrange("p t m i -> p m t i"),
-                 in_=wd_raw[g][:].rearrange("p i (m t) -> p m t i", t=4))
+        def quantise_wd(g, t0, t1, tag):
+            grouped = keep.tile([P, t1 - t0, P, 4], BF16, name="wd_bf", tag=tag, align_bytes=64)
+            nc.scalar.copy(out=grouped[:].rearrange("p t m i -> p m i t"),
+                           in_=wd_raw[g][:].rearrange("p i (m t) -> p m i t", t=4)[:, :, :, t0:t1])
+            cols = slice(t0 * P, t1 * P)
             nc.vector.quantize_mx(
-                out=wd_codes[:, g, :].bitcast(FP8X4), scales=wd_planes[:, g, :],
+                out=wd_codes[:, g, cols].bitcast(FP8X4), scales=wd_planes[:, g, cols],
                 in_=grouped[:].rearrange("p t m i -> p (t m i)"),
             )
 
@@ -154,12 +154,7 @@ def tile_list_competition_dispersal_kernel(
             half, c0 = divmod(blk * BLOCK, HALF)
             cols = slice(blk * BLOCK, (blk + 1) * BLOCK)
             words = picked[lst, a, half][:, c0 : c0 + BLOCK].bitcast(FP8X4)
-            if lst == 0:
-                plane = own_planes[4 * a : P, cols]
-            elif a == 0:
-                plane = fp4_planes[:, lst - 1, cols]
-            else:
-                plane = lifted[:, lst - 1, cols]
+            plane = (planes, lifted)[a][:, lst, cols]
             return words, plane
 
         def product(bank, terms, blk, start=True, stop=True):
@@ -221,7 +216,7 @@ def tile_list_competition_dispersal_kernel(
                 words = hs[blk].bitcast(F32)
                 for u in range(2):
                     nc.tensor.transpose(turned[:, b, u, :], words[:, u * P : (u + 1) * P], ident[:])
-            grouped = keep.tile([P, QUARTER * 4], BF16, name="h_grouped", tag="h%d" % (quarter + 1), align_bytes=64)
+            grouped = keep.tile([P, QUARTER * 4], BF16, name="h_grouped", tag="hg%d" % quarter, align_bytes=64)
             nc.scalar.copy(out=grouped[:].bitcast(F32).rearrange("p (b j u) -> p b j u", b=2, u=2),
                            in_=turned[:].rearrange("p b u j -> p b j u"))
             h_quant[quarter] = grouped
@@ -267,7 +262,7 @@ def tile_list_competition_dispersal_kernel(
         def regroup(quarter, g, cast):
             y = ys[quarter, g]
             grouped = ring.tile([P, QUARTER, 4], BF16, name="y_grouped", tag="y_grouped", bufs=8, align_bytes=64)
-            cast(out=grouped[:], in_=y[:].rearrange("p t j -> p j t"))
+            cast(out=grouped[:].rearrange("p (c n) t -> p c t n", n=4), in_=y[:].rearrange("p t (c n) -> p c t n", n=4))
             y_bf[quarter, g] = grouped
 
         def quantise_y(quarter, g):
@@ -288,23 +283,25 @@ def tile_list_competition_dispersal_kernel(
                 )
 
         on_s, on_v = nc.scalar.copy, nc.vector.tensor_copy
+        casts = (on_v, on_v, on_v, on_v, on_v, on_v, on_s, on_v)
 
-        def on_g(out, in_):
-            nc.gpsimd.tensor_scalar(out, in_, 1.0, 0.0, MULT, ADD)
+        def finish(quarter):
+            for g in range(GROUPS):
+                regroup(quarter, g, casts[2 * quarter + g])
+            for g in range(GROUPS):
+                quantise_y(quarter, g)
+            store_codes(quarter)
 
-        casts = (on_g, on_g, on_g, on_g, on_g, on_g, on_s, on_v)
-
-        for half in range(2):
-            for lst in (1, 0):
+        for lst in (1, 0, 2):
+            for half in range(2):
                 gather_words(lst, 0, half, "w%d0%d" % (lst, half))
-        gather_words(2, 0, 0, "w200")
         for half in range(2):
             for lst in (1, 0):
                 gather_words(lst, 1, half, "w%d1%d" % (lst, half))
-        quantise_ws(0)
-        gather_words(2, 1, 0, "ws_bf0")
-        quantise_ws(1)
-        gather_words(2, 0, 1, "ws_bf1")
+        for a in range(PASSES):
+            quantise_ws(a)
+            gather_words(2, 1, a, "ws_bf%d" % a)
+        quantise_wd(0, 0, 4, "wd0")
         for a in range(PASSES):
             for blk in range(8):
                 crowding(blk, a, a == 0)
@@ -313,38 +310,36 @@ def tile_list_competition_dispersal_kernel(
             predation(blk)
         growth(0)
         turn(0)
-        quantise_wd(0, on_g)
         quantise_h(0)
-        quantise_wd(1, on_g)
-        for blk in (4, 5):
-            abundance(blk)
+        quantise_wd(1, 0, 2, "wd1")
+        quantise_wd(1, 2, 4, "h0")
+        abundance(4)
+        abundance(5)
+        predation(4)
+        predation(5)
         disperse(0, 0, ())
         growth(1)
-        gather_words(2, 1, 1, "room3")
-        disperse(0, 1, ())
         turn(1)
         quantise_h(1)
-        for blk in (4, 5):
-            predation(blk)
-        for blk in (6, 7):
-            abundance(blk)
-            predation(blk)
+        abundance(6)
+        abundance(7)
+        disperse(0, 1, ())
+        predation(6)
+        predation(7)
         growth(2)
-        disperse(1, 0, ())
         turn(2)
         quantise_h(2)
+        disperse(1, 0, ())
         disperse(1, 1, ())
         growth(3)
-        disperse(2, 0, ())
         turn(3)
         quantise_h(3)
+        disperse(2, 0, ())
         disperse(2, 1, ())
         disperse(3, 0, ())
-        disperse(3, 1, (0, 1))
-        for quarter in range(4):
-            for g in range(GROUPS):
-                regroup(quarter, g, casts[2 * quarter + g])
-            for g in range(GROUPS):
-                quantise_y(quarter, g)
-            store_codes(quarter)
+        disperse(3, 1, ())
+        finish(0)
+        finish(1)
+        finish(2)
+        finish(3)
         store_scales()

@@ -163,12 +163,6 @@ def tile_list_competition_dispersal_kernel(
                 nc.tensor.matmul_mx(out=bank[:], lhsT=lhs, lhsT_scale=lhs_plane, rhs=words, rhs_scale=plane,
                                     start=(start and n == 0), stop=(stop and n == len(terms) - 1))
 
-        def dealt(ap):
-            return ap.rearrange("j (p u e) -> j u p e", u=2, e=2)
-
-        def pairs(ap):
-            return ap.rearrange("j (u p e) -> j u p e", u=2, e=2)
-
         room = {}
 
         c_banks = {}
@@ -181,7 +175,7 @@ def tile_list_competition_dispersal_kernel(
             product(c_banks[blk], terms, blk, start=first, stop=not first)
             if not first:
                 u = keep.tile([P, H], F32, name="room%d" % blk, tag="room%d" % blk, align_bytes=64)
-                nc.scalar.activation(out=pairs(u[:]), in_=dealt(c_banks[blk][:]), func=COPY, scale=-1.0, bias=1.0)
+                nc.scalar.activation(out=u[:], in_=c_banks[blk][:], func=COPY, scale=-1.0, bias=1.0)
                 room[blk] = u
 
         h_quant, h_rows = {}, {}
@@ -201,11 +195,11 @@ def tile_list_competition_dispersal_kernel(
             grown, hs = {}, {}
             for blk in blks:
                 grown[blk] = ring.tile([P, H], F32, name="grown", tag="grown")
-                nc.vector.tensor_tensor(pairs(grown[blk][:]), dealt(a_banks[blk][:]), pairs(room[blk][:]), MULT)
+                nc.vector.tensor_tensor(grown[blk][:], a_banks[blk][:], room[blk][:], MULT)
             both = keep.tile([P, 2, H], BF16, name="h_rows", tag="h%d" % quarter, align_bytes=64)
             for blk in blks:
                 hs[blk] = both[:, blk % 2, :]
-                nc.vector.tensor_tensor(pairs(hs[blk]), pairs(grown[blk][:]), dealt(p_banks[blk][:]), SUBTRACT)
+                nc.vector.tensor_tensor(hs[blk], grown[blk][:], p_banks[blk][:], SUBTRACT)
             h_rows[quarter] = hs
 
         def turn(quarter):
@@ -215,7 +209,7 @@ def tile_list_competition_dispersal_kernel(
             for b, blk in enumerate(blks):
                 words = hs[blk].bitcast(F32)
                 for u in range(2):
-                    nc.tensor.transpose(turned[:, b, u, :], words[:, u * P : (u + 1) * P], ident[:])
+                    nc.tensor.transpose(turned[:, b, u, :], words[:, u : 2 * P : 2], ident[:])
             grouped = keep.tile([P, QUARTER * 4], BF16, name="h_grouped", tag="hg%d" % quarter, align_bytes=64)
             nc.scalar.copy(out=grouped[:].bitcast(F32).rearrange("p (b j u) -> p b j u", b=2, u=2),
                            in_=turned[:].rearrange("p b u j -> p b j u"))

@@ -25,7 +25,6 @@ HALF = 512
 BLOCK = 128
 QUARTER = 256
 GROUPS = 2
-EARLY = 3 * QUARTER
 
 
 def tile_list_competition_dispersal_kernel(
@@ -36,7 +35,7 @@ def tile_list_competition_dispersal_kernel(
     with ExitStack() as ctx:
         keep = ctx.enter_context(tc.tile_pool(name="keep", bufs=1))
         ring = ctx.enter_context(tc.tile_pool(name="ring", bufs=2))
-        psum = ctx.enter_context(tc.psum_pool(name="psum", bufs=8))
+        psum = ctx.enter_context(tc.psum_pool(name="psum", bufs=1))
 
         tab_plane = keep.tile([P, T], U8, name="tab_plane", align_bytes=64)
         nc.vector.memset(tab_plane[:, 0:2816].bitcast(I32), 0)
@@ -45,13 +44,17 @@ def tile_list_competition_dispersal_kernel(
         for n, src in enumerate((offs, offs2, offs3)):
             lst = keep.tile([P, S // 16], U16, name="list%d" % n)
             lists.append(lst)
-        for n in range(3):
-            nc.sync.dma_start(lists[n][:], (offs, offs2, offs3)[n])
+        nc.sync.dma_start(lists[1][:], offs2)
+        staged = keep.tile([16, 3, PASSES, H], U8, name="staged", align_bytes=64)
+        for w, src in enumerate((wi_scales, wc_scales, wp_scales)):
+            nc.sync.dma_start(out=staged[:, w, :, :].bitcast(I32), in_=src.rearrange("a q c -> q a c").bitcast(I32))
         for r in range(4):
             nc.sync.dma_start(
                 out=tab_plane[r:P:16, :].bitcast(I32),
                 in_=tab_scales.rearrange("a (q r) t -> r q a t", r=4)[r].bitcast(I32),
             )
+        nc.sync.dma_start(lists[0][:], offs)
+        nc.sync.dma_start(lists[2][:], offs3)
         tab = []
 
         def load_table(a):
@@ -60,14 +63,6 @@ def tile_list_competition_dispersal_kernel(
             tab.append(words)
 
         load_table(0)
-        w_planes = keep.tile([P, 3, PASSES, H], U8, name="w_planes", align_bytes=64)
-        nc.gpsimd.memset(w_planes[:].rearrange("p w a c -> p (w a c)").bitcast(I32), 0)
-        for w, src in enumerate((wi_scales, wc_scales, wp_scales)):
-            nc.sync.dma_start(
-                out=w_planes[0:16, w, :, :].bitcast(I32),
-                in_=src.rearrange("a q c -> q a c").bitcast(I32),
-            )
-        load_table(1)
         wc = keep.tile([P, PASSES, 2 * H], U8, name="wc", align_bytes=64)
         nc.sync.dma_start(out=wc[:].bitcast(I32), in_=wc_words.rearrange("a p c -> p a c").bitcast(I32))
         wi = []
@@ -78,10 +73,16 @@ def tile_list_competition_dispersal_kernel(
             wi.append(words)
 
         load_wi(0)
+        w_planes = keep.tile([P, 3, PASSES, H], U8, name="w_planes", align_bytes=64)
+        flat_planes = w_planes[:].rearrange("p w a c -> p (w a c)").bitcast(I32)
+        flat_staged = staged[:].rearrange("p w a c -> p (w a c)").bitcast(I32)
+        nc.gpsimd.memset(flat_planes, 0)
+        for r in range(4):
+            nc.sync.dma_start(out=flat_planes[r:P:32, :], in_=flat_staged[r:16:4, :])
         ws_raw, wd_raw = [], []
 
         def load_ws(a):
-            raw = keep.tile([P, 4, H], F32, name="ws_raw%d" % a)
+            raw = keep.tile([P, 4, H], F32, name="ws_raw%d" % a, tag="ws_raw%d" % a, align_bytes=64)
             nc.sync.dma_start(out=raw[:], in_=ws[512 * a : 512 * (a + 1), :].rearrange("(p i) c -> p i c", i=4))
             ws_raw.append(raw)
 
@@ -91,9 +92,10 @@ def tile_list_competition_dispersal_kernel(
             wd_raw.append(raw)
 
         load_ws(0)
+        load_table(1)
 
         planes = keep.tile([P, 3, S], U8, name="planes", align_bytes=64)
-        for lst in range(3):
+        for lst in (1, 0, 2):
             nc.vector.tensor_copy(planes[:, lst, :], tab_plane[:].indirect(lists[lst][:]))
         lifted = keep.tile([P, 3, S], U8, name="lifted", align_bytes=64)
         nc.gpsimd.memset(lifted[:].rearrange("p l s -> p (l s)").bitcast(I32), 0)
@@ -101,17 +103,14 @@ def tile_list_competition_dispersal_kernel(
             out=lifted[0:112].rearrange("p l s -> p (l s)").bitcast(I32),
             in_=planes[16:128].rearrange("p l s -> p (l s)").bitcast(I32),
         )
-        load_wi(1)
-        gains = keep.tile([P, GROUPS, 4], F32, name="gains")
-        nc.sync.dma_start(out=gains[:], in_=gain.rearrange("(g p t) -> p g t", g=GROUPS, t=4))
-        flat_planes = w_planes[:].rearrange("p w a c -> p (w a c)").bitcast(I32)
-        for q in range(1, 4):
-            nc.sync.dma_start(out=flat_planes[32 * q : 32 * q + 4, :], in_=flat_planes[4 * q : 4 * q + 4, :])
 
+        load_wi(1)
         load_ws(1)
-        load_wd(0)
         wp = keep.tile([P, PASSES, 2 * H], U8, name="wp", align_bytes=64)
         nc.sync.dma_start(out=wp[:].bitcast(I32), in_=wp_words.rearrange("a p c -> p a c").bitcast(I32))
+        load_wd(0)
+        gains = keep.tile([P, GROUPS, 4], F32, name="gains")
+        nc.sync.dma_start(out=gains[:], in_=gain.rearrange("(g p t) -> p g t", g=GROUPS, t=4))
         load_wd(1)
 
         ident = keep.tile([P, P], F32, name="ident")
@@ -123,7 +122,13 @@ def tile_list_competition_dispersal_kernel(
             words = keep.tile([P, HALF], U32, name="picked_%d_%d_%d" % (lst, a, half), tag=tag, align_bytes=64)
             cols = slice(half * HALF // 16, (half + 1) * HALF // 16)
             nc.vector.tensor_copy(words[:], tab[a][:].bitcast(U32).indirect(lists[lst][:, cols]))
-            picked[lst, a, half] = words
+            picked[lst, a, half] = words[:]
+
+        def gather_whole(lst, a, tag):
+            words = keep.tile([P, S], U32, name="picked_%d_%d" % (lst, a), tag=tag, align_bytes=64)
+            nc.vector.tensor_copy(words[:], tab[a][:].bitcast(U32).indirect(lists[lst][:]))
+            for half in range(2):
+                picked[lst, a, half] = words[:, half * HALF : (half + 1) * HALF]
 
         ws_codes = keep.tile([P, PASSES, H], U32, name="ws_codes", align_bytes=64)
         ws_planes = keep.tile([P, PASSES, H], U8, align_bytes=64)
@@ -163,31 +168,38 @@ def tile_list_competition_dispersal_kernel(
                 nc.tensor.matmul_mx(out=bank[:], lhsT=lhs, lhsT_scale=lhs_plane, rhs=words, rhs_scale=plane,
                                     start=(start and n == 0), stop=(stop and n == len(terms) - 1))
 
-        room = {}
+        room, c_banks = {}, {}
 
-        c_banks = {}
+        def new_bank(shape, name, b):
+            return psum.tile(shape, F32, name=name, tag="bank%d" % b)
 
-        def crowding(blk, a, first):
+        def crowding(blk, lst, a):
+            first, last = (lst, a) == (1, 0), (lst, a) == (0, 1)
             if first:
-                c_banks[blk] = psum.tile([P, H], F32, name="crowd_bank", tag="bank")
-            terms = [(1, a, wc[:, a, :].bitcast(FP4X4), w_planes[:, 1, a, :]),
-                     (0, a, wi[a][:].bitcast(FP8X4), w_planes[:, 0, a, :])]
-            product(c_banks[blk], terms, blk, start=first, stop=not first)
-            if not first:
-                u = keep.tile([P, H], F32, name="room%d" % blk, tag="room%d" % blk, align_bytes=64)
-                nc.scalar.activation(out=u[:], in_=c_banks[blk][:], func=COPY, scale=-1.0, bias=1.0)
-                room[blk] = u
+                c_banks[blk] = new_bank([P, H], "crowd_bank", blk)
+            if lst == 1:
+                term = (1, a, wc[:, a, :].bitcast(FP4X4), w_planes[:, 1, a, :])
+            else:
+                term = (0, a, wi[a][:].bitcast(FP8X4), w_planes[:, 0, a, :])
+            product(c_banks[blk], [term], blk, start=first, stop=last)
+
+        def make_room():
+            first = keep.tile([P, H], F32, name="room0", tag="wd0", align_bytes=64)
+            rest = keep.tile([P, 7, H], F32, name="room", tag="ws_raw1", align_bytes=64)
+            for blk in range(8):
+                room[blk] = first[:] if blk == 0 else rest[:, blk - 1, :]
+                nc.scalar.activation(out=room[blk], in_=c_banks[blk][:], func=COPY, scale=-1.0, bias=1.0)
 
         h_quant, h_rows = {}, {}
 
         a_banks, p_banks = {}, {}
 
-        def abundance(blk):
-            a_banks[blk] = psum.tile([P, H], F32, name="a_bank", tag="bank")
+        def abundance(blk, b):
+            a_banks[blk] = new_bank([P, H], "a_bank", b)
             product(a_banks[blk], [(0, a, ws_codes[:, a, :].bitcast(FP8X4), ws_planes[:, a, :]) for a in range(PASSES)], blk)
 
-        def predation(blk):
-            p_banks[blk] = psum.tile([P, H], F32, name="p_bank", tag="bank")
+        def predation(blk, b):
+            p_banks[blk] = new_bank([P, H], "p_bank", b)
             product(p_banks[blk], [(2, a, wp[:, a, :].bitcast(FP4X4), w_planes[:, 2, a, :]) for a in range(PASSES)], blk)
 
         def growth(quarter):
@@ -195,17 +207,17 @@ def tile_list_competition_dispersal_kernel(
             grown, hs = {}, {}
             for blk in blks:
                 grown[blk] = ring.tile([P, H], F32, name="grown", tag="grown")
-                nc.vector.tensor_tensor(grown[blk][:], a_banks[blk][:], room[blk][:], MULT)
+                nc.vector.tensor_tensor(grown[blk][:], a_banks[blk][:], room[blk], MULT)
             both = keep.tile([P, 2, H], BF16, name="h_rows", tag="h%d" % quarter, align_bytes=64)
             for blk in blks:
                 hs[blk] = both[:, blk % 2, :]
                 nc.vector.tensor_tensor(hs[blk], grown[blk][:], p_banks[blk][:], SUBTRACT)
             h_rows[quarter] = hs
 
-        def turn(quarter):
+        def turn(quarter, bank_no):
             blks = (2 * quarter, 2 * quarter + 1)
             hs = h_rows[quarter]
-            turned = psum.tile([P, 2, 2, BLOCK], F32, name="turned", tag="bank")
+            turned = new_bank([P, 2, 2, BLOCK], "turned", bank_no)
             for b, blk in enumerate(blks):
                 words = hs[blk].bitcast(F32)
                 for u in range(2):
@@ -224,12 +236,12 @@ def tile_list_competition_dispersal_kernel(
             nc.vector.quantize_mx(out=codes[:].bitcast(FP8X4), scales=plane[:], in_=h_quant[quarter][:])
             h_codes[quarter] = (codes, plane)
 
-        def disperse(quarter, g, on_vector):
+        def disperse(quarter, g, banks, on_vector=()):
             cols = slice(quarter * QUARTER, (quarter + 1) * QUARTER)
             codes, plane = h_codes[quarter]
             y = ring.tile([P, 4, QUARTER], F32, name="y", tag="y", bufs=8)
             for pair in range(2):
-                bank = psum.tile([P, 2, QUARTER], F32, name="y_bank", tag="bank")
+                bank = new_bank([P, 2, QUARTER], "y_bank", banks[pair])
                 for e in range(2):
                     t = 2 * pair + e
                     nc.tensor.matmul_mx(
@@ -277,7 +289,7 @@ def tile_list_competition_dispersal_kernel(
                 )
 
         on_s, on_v = nc.scalar.copy, nc.vector.tensor_copy
-        casts = (on_v, on_v, on_v, on_v, on_v, on_v, on_s, on_v)
+        casts = (on_v, on_v, on_v, on_v, on_v, on_v, on_v, on_v)
 
         def finish(quarter):
             for g in range(GROUPS):
@@ -286,52 +298,58 @@ def tile_list_competition_dispersal_kernel(
                 quantise_y(quarter, g)
             store_codes(quarter)
 
-        for lst in (1, 0, 2):
-            for half in range(2):
-                gather_words(lst, 0, half, "w%d0%d" % (lst, half))
+        gather_whole(1, 0, "w10")
+        gather_whole(0, 0, "w00")
+        quantise_ws(0)
+        gather_whole(2, 0, "w20")
         for half in range(2):
             for lst in (1, 0):
                 gather_words(lst, 1, half, "w%d1%d" % (lst, half))
-        for a in range(PASSES):
-            quantise_ws(a)
-            gather_words(2, 1, a, "ws_bf%d" % a)
-        quantise_wd(0, 0, 4, "wd0")
-        for a in range(PASSES):
+        quantise_ws(1)
+        gather_words(2, 1, 0, "ws_bf1")
+        gather_words(2, 1, 1, "ws_bf0")
+        for lst in (1, 0):
             for blk in range(8):
-                crowding(blk, a, a == 0)
+                crowding(blk, lst, 0)
+        for half in range(2):
+            for lst in (1, 0):
+                for blk in range(4 * half, 4 * half + 4):
+                    crowding(blk, lst, 1)
+        make_room()
         for blk in range(4):
-            abundance(blk)
-            predation(blk)
+            abundance(blk, blk)
+        for blk in range(4):
+            predation(blk, 4 + blk)
         growth(0)
-        turn(0)
+        quantise_wd(0, 0, 4, "wd0")
+        turn(0, 0)
         quantise_h(0)
-        quantise_wd(1, 0, 2, "wd1")
-        quantise_wd(1, 2, 4, "h0")
-        abundance(4)
-        abundance(5)
-        predation(4)
-        predation(5)
-        disperse(0, 0, ())
+        quantise_wd(1, 0, 4, "h0")
+        abundance(4, 1)
+        abundance(5, 4)
+        disperse(0, 0, (5, 0))
         growth(1)
-        turn(1)
+        turn(1, 2)
         quantise_h(1)
-        abundance(6)
-        abundance(7)
-        disperse(0, 1, ())
-        predation(6)
-        predation(7)
+        predation(4, 3)
+        predation(5, 6)
+        disperse(0, 1, (7, 5))
         growth(2)
-        turn(2)
+        abundance(6, 1)
+        abundance(7, 4)
+        predation(6, 3)
+        predation(7, 6)
+        disperse(1, 0, (2, 0))
+        turn(2, 7)
         quantise_h(2)
-        disperse(1, 0, ())
-        disperse(1, 1, ())
+        disperse(1, 1, (5, 2))
         growth(3)
-        turn(3)
+        turn(3, 1)
         quantise_h(3)
-        disperse(2, 0, ())
-        disperse(2, 1, ())
-        disperse(3, 0, ())
-        disperse(3, 1, ())
+        disperse(2, 0, (0, 7))
+        disperse(2, 1, (5, 2))
+        disperse(3, 0, (4, 3))
+        disperse(3, 1, (6, 0))
         finish(0)
         finish(1)
         finish(2)

@@ -91,7 +91,6 @@ def tile_list_competition_dispersal_kernel(
             nc.sync.dma_start(out=raw[:], in_=wd[:, 512 * g : 512 * (g + 1)].rearrange("(p i) n -> p i n", i=4))
             wd_raw.append(raw)
 
-        load_ws(0)
         load_table(1)
 
         planes = keep.tile([P, 3, S], U8, name="planes", align_bytes=64)
@@ -105,6 +104,7 @@ def tile_list_competition_dispersal_kernel(
         )
 
         load_wi(1)
+        load_ws(0)
         load_ws(1)
         wp = keep.tile([P, PASSES, 2 * H], U8, name="wp", align_bytes=64)
         nc.sync.dma_start(out=wp[:].bitcast(I32), in_=wp_words.rearrange("a p c -> p a c").bitcast(I32))
@@ -124,22 +124,21 @@ def tile_list_competition_dispersal_kernel(
             nc.vector.tensor_copy(words[:], tab[a][:].bitcast(U32).indirect(lists[lst][:, cols]))
             picked[lst, a, half] = words[:]
 
-        def gather_whole(lst, a, tag):
-            words = keep.tile([P, S], U32, name="picked_%d_%d" % (lst, a), tag=tag, align_bytes=64)
-            nc.vector.tensor_copy(words[:], tab[a][:].bitcast(U32).indirect(lists[lst][:]))
-            for half in range(2):
-                picked[lst, a, half] = words[:, half * HALF : (half + 1) * HALF]
-
         ws_codes = keep.tile([P, PASSES, H], U32, name="ws_codes", align_bytes=64)
         ws_planes = keep.tile([P, PASSES, H], U8, align_bytes=64)
 
-        def quantise_ws(a):
+        ws_bf = {}
+
+        def round_ws(a, cast):
             grouped = keep.tile([P, H, 4], BF16, name="ws_bf%d" % a, tag="ws_bf%d" % a, align_bytes=64)
-            nc.scalar.copy(out=grouped[:].rearrange("p (c n) i -> p c i n", n=4),
-                           in_=ws_raw[a][:].rearrange("p i (c n) -> p c i n", n=4))
+            cast(out=grouped[:].rearrange("p (c n) i -> p c i n", n=4),
+                 in_=ws_raw[a][:].rearrange("p i (c n) -> p c i n", n=4))
+            ws_bf[a] = grouped
+
+        def quantise_ws(a):
             nc.vector.quantize_mx(
                 out=ws_codes[:, a, :].bitcast(FP8X4), scales=ws_planes[:, a, :],
-                in_=grouped[:].rearrange("p c i -> p (c i)"),
+                in_=ws_bf[a][:].rearrange("p c i -> p (c i)"),
             )
 
         wd_codes = keep.tile([P, GROUPS, 512], U32, name="wd_codes", align_bytes=64)
@@ -183,12 +182,20 @@ def tile_list_competition_dispersal_kernel(
                 term = (0, a, wi[a][:].bitcast(FP8X4), w_planes[:, 0, a, :])
             product(c_banks[blk], [term], blk, start=first, stop=last)
 
-        def make_room():
-            first = keep.tile([P, H], F32, name="room0", tag="wd0", align_bytes=64)
-            rest = keep.tile([P, 7, H], F32, name="room", tag="ws_raw1", align_bytes=64)
+        def by_word(rows):
+            return rows.rearrange("j (p u e) -> j u p e", u=2, e=2)
+
+        def as_words(rows):
+            return rows.rearrange("j (u p e) -> j u p e", u=2, e=2)
+
+        def make_rooms():
+            later = keep.tile([P, 6, H], F32, name="rooms", tag="ws_raw0", align_bytes=64)
             for blk in range(8):
-                room[blk] = first[:] if blk == 0 else rest[:, blk - 1, :]
-                nc.scalar.activation(out=room[blk], in_=c_banks[blk][:], func=COPY, scale=-1.0, bias=1.0)
+                if blk < 2:
+                    room[blk] = keep.tile([P, H], F32, name="room%d" % blk, align_bytes=64)[:]
+                else:
+                    room[blk] = later[:, blk - 2, :]
+                nc.scalar.activation(out=as_words(room[blk]), in_=by_word(c_banks[blk][:]), func=COPY, scale=-1.0, bias=1.0)
 
         h_quant, h_rows = {}, {}
 
@@ -207,11 +214,11 @@ def tile_list_competition_dispersal_kernel(
             grown, hs = {}, {}
             for blk in blks:
                 grown[blk] = ring.tile([P, H], F32, name="grown", tag="grown")
-                nc.vector.tensor_tensor(grown[blk][:], a_banks[blk][:], room[blk], MULT)
+                nc.vector.tensor_tensor(as_words(grown[blk][:]), by_word(a_banks[blk][:]), as_words(room[blk]), MULT)
             both = keep.tile([P, 2, H], BF16, name="h_rows", tag="h%d" % quarter, align_bytes=64)
             for blk in blks:
                 hs[blk] = both[:, blk % 2, :]
-                nc.vector.tensor_tensor(hs[blk], grown[blk][:], p_banks[blk][:], SUBTRACT)
+                nc.vector.tensor_tensor(as_words(hs[blk]), as_words(grown[blk][:]), by_word(p_banks[blk][:]), SUBTRACT)
             h_rows[quarter] = hs
 
         def turn(quarter, bank_no):
@@ -221,7 +228,7 @@ def tile_list_competition_dispersal_kernel(
             for b, blk in enumerate(blks):
                 words = hs[blk].bitcast(F32)
                 for u in range(2):
-                    nc.tensor.transpose(turned[:, b, u, :], words[:, u : 2 * P : 2], ident[:])
+                    nc.tensor.transpose(turned[:, b, u, :], words[:, u * P : (u + 1) * P], ident[:])
             grouped = keep.tile([P, QUARTER * 4], BF16, name="h_grouped", tag="hg%d" % quarter, align_bytes=64)
             nc.scalar.copy(out=grouped[:].bitcast(F32).rearrange("p (b j u) -> p b j u", b=2, u=2),
                            in_=turned[:].rearrange("p b u j -> p b j u"))
@@ -281,11 +288,11 @@ def tile_list_competition_dispersal_kernel(
             nc.sync.dma_start(
                 out=out_1[:, :, cols, :].rearrange("g p m t -> p g (m t)").bitcast(I32), in_=y_codes[quarter][:].bitcast(I32))
 
-        def store_scales():
-            for q in range(4):
+        def store_scales(cols):
+            for r in range(4):
                 nc.sync.dma_start(
-                    out=out_2[:, 4 * q : 4 * q + 4, :].rearrange("g r m -> r g m").bitcast(I32),
-                    in_=y_planes[32 * q : 32 * q + 4, :, :].bitcast(I32),
+                    out=out_2[:, r:16:4, cols].rearrange("g q m -> q g m").bitcast(I32),
+                    in_=y_planes[r:P:32, :, cols].bitcast(I32),
                 )
 
         on_s, on_v = nc.scalar.copy, nc.vector.tensor_copy
@@ -298,60 +305,64 @@ def tile_list_competition_dispersal_kernel(
                 quantise_y(quarter, g)
             store_codes(quarter)
 
-        gather_whole(1, 0, "w10")
-        gather_whole(0, 0, "w00")
-        quantise_ws(0)
-        gather_whole(2, 0, "w20")
+        for half in range(2):
+            for lst in (1, 0):
+                gather_words(lst, 0, half, "w%d0%d" % (lst, half))
+        gather_words(2, 0, 0, "w200")
         for half in range(2):
             for lst in (1, 0):
                 gather_words(lst, 1, half, "w%d1%d" % (lst, half))
+        gather_words(2, 1, 0, "w210")
+        round_ws(0, on_s)
+        round_ws(1, on_v)
+        quantise_ws(0)
         quantise_ws(1)
-        gather_words(2, 1, 0, "ws_bf1")
-        gather_words(2, 1, 1, "ws_bf0")
-        for lst in (1, 0):
-            for blk in range(8):
-                crowding(blk, lst, 0)
-        for half in range(2):
-            for lst in (1, 0):
-                for blk in range(4 * half, 4 * half + 4):
-                    crowding(blk, lst, 1)
-        make_room()
+        gather_words(2, 0, 1, "ws_bf1")
+        for a in range(PASSES):
+            for half in range(2):
+                for lst in (1, 0):
+                    for blk in range(4 * half, 4 * half + 4):
+                        crowding(blk, lst, a)
+        make_rooms()
+        predation(0, 0)
+        predation(1, 1)
         for blk in range(4):
-            abundance(blk, blk)
-        for blk in range(4):
-            predation(blk, 4 + blk)
-        growth(0)
+            abundance(blk, 2 + blk)
+        predation(2, 6)
+        predation(3, 7)
         quantise_wd(0, 0, 4, "wd0")
-        turn(0, 0)
+        growth(0)
+        gather_words(2, 1, 1, "room1")
+        turn(0, 2)
         quantise_h(0)
         quantise_wd(1, 0, 4, "h0")
-        abundance(4, 1)
-        abundance(5, 4)
-        disperse(0, 0, (5, 0))
+        abundance(4, 3)
+        abundance(5, 0)
         growth(1)
-        turn(1, 2)
+        disperse(0, 0, (1, 2))
+        turn(1, 4)
         quantise_h(1)
-        predation(4, 3)
+        predation(4, 5)
         predation(5, 6)
-        disperse(0, 1, (7, 5))
+        disperse(0, 1, (7, 1))
         growth(2)
-        abundance(6, 1)
-        abundance(7, 4)
-        predation(6, 3)
-        predation(7, 6)
-        disperse(1, 0, (2, 0))
-        turn(2, 7)
+        abundance(6, 4)
+        abundance(7, 3)
+        disperse(1, 0, (2, 7))
+        predation(6, 0)
+        predation(7, 5)
+        turn(2, 6)
         quantise_h(2)
-        disperse(1, 1, (5, 2))
+        disperse(1, 1, (1, 2))
         growth(3)
-        turn(3, 1)
+        turn(3, 7)
         quantise_h(3)
-        disperse(2, 0, (0, 7))
-        disperse(2, 1, (5, 2))
-        disperse(3, 0, (4, 3))
-        disperse(3, 1, (6, 0))
+        disperse(2, 0, (6, 1))
+        disperse(2, 1, (2, 4))
+        disperse(3, 0, (3, 0))
+        disperse(3, 1, (5, 7))
         finish(0)
         finish(1)
         finish(2)
         finish(3)
-        store_scales()
+        store_scales(slice(0, S))

@@ -38,8 +38,7 @@ def tile_list_competition_dispersal_kernel(
         psum = ctx.enter_context(tc.psum_pool(name="psum", bufs=1))
 
         tab_plane = keep.tile([P, T], U8, name="tab_plane", align_bytes=64)
-        nc.vector.memset(tab_plane[:, 0:2816].bitcast(I32), 0)
-        nc.gpsimd.memset(tab_plane[:, 2816:T].bitcast(I32), 0)
+        nc.vector.memset(tab_plane[:].bitcast(I32), 0)
         lists = []
         for n, src in enumerate((offs, offs2, offs3)):
             lst = keep.tile([P, S // 16], U16, name="list%d" % n)
@@ -76,7 +75,7 @@ def tile_list_competition_dispersal_kernel(
         w_planes = keep.tile([P, 3, PASSES, H], U8, name="w_planes", align_bytes=64)
         flat_planes = w_planes[:].rearrange("p w a c -> p (w a c)").bitcast(I32)
         flat_staged = staged[:].rearrange("p w a c -> p (w a c)").bitcast(I32)
-        nc.gpsimd.memset(flat_planes, 0)
+        nc.vector.memset(flat_planes, 0)
         for r in range(4):
             nc.sync.dma_start(out=flat_planes[r:P:32, :], in_=flat_staged[r:16:4, :])
         ws_raw, wd_raw = [], []
@@ -97,7 +96,7 @@ def tile_list_competition_dispersal_kernel(
         for lst in (1, 0, 2):
             nc.vector.tensor_copy(planes[:, lst, :], tab_plane[:].indirect(lists[lst][:]))
         lifted = keep.tile([P, 3, S], U8, name="lifted", align_bytes=64)
-        nc.gpsimd.memset(lifted[:].rearrange("p l s -> p (l s)").bitcast(I32), 0)
+        nc.vector.memset(lifted[:].rearrange("p l s -> p (l s)").bitcast(I32), 0)
         nc.sync.dma_start(
             out=lifted[0:112].rearrange("p l s -> p (l s)").bitcast(I32),
             in_=planes[16:128].rearrange("p l s -> p (l s)").bitcast(I32),

@@ -16,15 +16,21 @@ FP8X4 = mybir.dt.float8_e4m3fn_x4
 FP4X4 = mybir.dt.float4_e2m1fn_x4
 COPY = mybir.ActivationFunctionType.Copy
 MULT = mybir.AluOpType.mult
-ADD = mybir.AluOpType.add
 SUBTRACT = mybir.AluOpType.subtract
 
 P = 128
-PASSES = 2
+PASS_ROWS = 512
+PASSES = K // PASS_ROWS
+GROUPS = N // PASS_ROWS
 HALF = 512
-BLOCK = 128
 QUARTER = 256
-GROUPS = 2
+BLOCK = 128
+BLOCKS = S // BLOCK
+QUARTERS = S // QUARTER
+BANKS = 8
+PER_COLUMN = 16
+SECOND_PASS = 16
+SPECIES, COMPETITOR, PREDATOR = 0, 1, 2
 
 
 def tile_list_competition_dispersal_kernel(
@@ -39,38 +45,50 @@ def tile_list_competition_dispersal_kernel(
 
         tab_plane = keep.tile([P, T], U8, name="tab_plane", align_bytes=64)
         nc.vector.memset(tab_plane[:].bitcast(I32), 0)
-        lists = []
-        for n, src in enumerate((offs, offs2, offs3)):
-            lst = keep.tile([P, S // 16], U16, name="list%d" % n)
-            lists.append(lst)
-        nc.sync.dma_start(lists[1][:], offs2)
+        lists = [keep.tile([P, S // PER_COLUMN], U16, name="list%d" % n) for n in range(3)]
+        nc.sync.dma_start(lists[COMPETITOR][:], offs2)
         staged = keep.tile([16, 3, PASSES, H], U8, name="staged", align_bytes=64)
         for w, src in enumerate((wi_scales, wc_scales, wp_scales)):
             nc.sync.dma_start(out=staged[:, w, :, :].bitcast(I32), in_=src.rearrange("a q c -> q a c").bitcast(I32))
         for r in range(4):
             nc.sync.dma_start(
-                out=tab_plane[r:P:16, :].bitcast(I32),
+                out=tab_plane[r:P:SECOND_PASS, :].bitcast(I32),
                 in_=tab_scales.rearrange("a (q r) t -> r q a t", r=4)[r].bitcast(I32),
             )
-        nc.sync.dma_start(lists[0][:], offs)
-        nc.sync.dma_start(lists[2][:], offs3)
-        tab = []
+        nc.sync.dma_start(lists[SPECIES][:], offs)
+        nc.sync.dma_start(lists[PREDATOR][:], offs3)
+
+        tab, wi, ws_raw, wd_raw = [], [], [], []
 
         def load_table(a):
             words = keep.tile([P, T], I32, name="tab%d" % a, align_bytes=64)
             nc.sync.dma_start(out=words[:], in_=tab_words[a].rearrange("p t i -> p (t i)").bitcast(I32))
             tab.append(words)
 
-        load_table(0)
-        wc = keep.tile([P, PASSES, 2 * H], U8, name="wc", align_bytes=64)
-        nc.sync.dma_start(out=wc[:].bitcast(I32), in_=wc_words.rearrange("a p c -> p a c").bitcast(I32))
-        wi = []
-
         def load_wi(a):
             words = keep.tile([P, H], I32, name="wi%d" % a, align_bytes=64)
             nc.sync.dma_start(out=words[:], in_=wi_words[a].rearrange("p c i -> p (c i)").bitcast(I32))
             wi.append(words)
 
+        def load_fp4(name, src):
+            words = keep.tile([P, PASSES, 2 * H], U8, name=name, align_bytes=64)
+            nc.sync.dma_start(out=words[:].bitcast(I32), in_=src.rearrange("a p c -> p a c").bitcast(I32))
+            return words
+
+        def load_ws(a):
+            raw = keep.tile([P, 4, H], F32, name="ws_raw%d" % a, tag="ws_raw%d" % a, align_bytes=64)
+            rows = ws[PASS_ROWS * a : PASS_ROWS * (a + 1), :]
+            nc.sync.dma_start(out=raw[:], in_=rows.rearrange("(p i) c -> p i c", i=4))
+            ws_raw.append(raw)
+
+        def load_wd(g):
+            raw = keep.tile([P, 4, PASS_ROWS], F32, name="wd_raw%d" % g)
+            cols = wd[:, PASS_ROWS * g : PASS_ROWS * (g + 1)]
+            nc.sync.dma_start(out=raw[:], in_=cols.rearrange("(p i) n -> p i n", i=4))
+            wd_raw.append(raw)
+
+        load_table(0)
+        wc = load_fp4("wc", wc_words)
         load_wi(0)
         w_planes = keep.tile([P, 3, PASSES, H], U8, name="w_planes", align_bytes=64)
         flat_planes = w_planes[:].rearrange("p w a c -> p (w a c)").bitcast(I32)
@@ -78,59 +96,46 @@ def tile_list_competition_dispersal_kernel(
         nc.vector.memset(flat_planes, 0)
         for r in range(4):
             nc.sync.dma_start(out=flat_planes[r:P:32, :], in_=flat_staged[r:16:4, :])
-        ws_raw, wd_raw = [], []
-
-        def load_ws(a):
-            raw = keep.tile([P, 4, H], F32, name="ws_raw%d" % a, tag="ws_raw%d" % a, align_bytes=64)
-            nc.sync.dma_start(out=raw[:], in_=ws[512 * a : 512 * (a + 1), :].rearrange("(p i) c -> p i c", i=4))
-            ws_raw.append(raw)
-
-        def load_wd(g):
-            raw = keep.tile([P, 4, 512], F32, name="wd_raw%d" % g)
-            nc.sync.dma_start(out=raw[:], in_=wd[:, 512 * g : 512 * (g + 1)].rearrange("(p i) n -> p i n", i=4))
-            wd_raw.append(raw)
-
         load_table(1)
 
         planes = keep.tile([P, 3, S], U8, name="planes", align_bytes=64)
-        for lst in (1, 0, 2):
+        for lst in (COMPETITOR, SPECIES, PREDATOR):
             nc.vector.tensor_copy(planes[:, lst, :], tab_plane[:].indirect(lists[lst][:]))
         lifted = keep.tile([P, 3, S], U8, name="lifted", align_bytes=64)
         nc.vector.memset(lifted[:].rearrange("p l s -> p (l s)").bitcast(I32), 0)
         nc.sync.dma_start(
-            out=lifted[0:112].rearrange("p l s -> p (l s)").bitcast(I32),
-            in_=planes[16:128].rearrange("p l s -> p (l s)").bitcast(I32),
+            out=lifted[0 : P - SECOND_PASS].rearrange("p l s -> p (l s)").bitcast(I32),
+            in_=planes[SECOND_PASS:P].rearrange("p l s -> p (l s)").bitcast(I32),
         )
 
         load_wi(1)
         load_ws(0)
         load_ws(1)
-        wp = keep.tile([P, PASSES, 2 * H], U8, name="wp", align_bytes=64)
-        nc.sync.dma_start(out=wp[:].bitcast(I32), in_=wp_words.rearrange("a p c -> p a c").bitcast(I32))
+        wp = load_fp4("wp", wp_words)
         load_wd(0)
         gains = keep.tile([P, GROUPS, 4], F32, name="gains")
         nc.sync.dma_start(out=gains[:], in_=gain.rearrange("(g p t) -> p g t", g=GROUPS, t=4))
         load_wd(1)
 
         ident = keep.tile([P, P], F32, name="ident")
-        make_identity(nc, ident[:])
+        nc.vector.memset(ident[:], 0.0)
+        make_identity(nc, ident[:], nomemset=True)
 
         picked = {}
 
         def gather_words(lst, a, half, tag):
             words = keep.tile([P, HALF], U32, name="picked_%d_%d_%d" % (lst, a, half), tag=tag, align_bytes=64)
-            cols = slice(half * HALF // 16, (half + 1) * HALF // 16)
+            cols = slice(half * HALF // PER_COLUMN, (half + 1) * HALF // PER_COLUMN)
             nc.vector.tensor_copy(words[:], tab[a][:].bitcast(U32).indirect(lists[lst][:, cols]))
             picked[lst, a, half] = words[:]
 
         ws_codes = keep.tile([P, PASSES, H], U32, name="ws_codes", align_bytes=64)
         ws_planes = keep.tile([P, PASSES, H], U8, align_bytes=64)
-
         ws_bf = {}
 
-        def round_ws(a, cast):
+        def round_ws(a, copy):
             grouped = keep.tile([P, H, 4], BF16, name="ws_bf%d" % a, tag="ws_bf%d" % a, align_bytes=64)
-            cast(out=grouped[:].rearrange("p (c n) i -> p c i n", n=4),
+            copy(out=grouped[:].rearrange("p (c n) i -> p c i n", n=4),
                  in_=ws_raw[a][:].rearrange("p i (c n) -> p c i n", n=4))
             ws_bf[a] = grouped
 
@@ -140,114 +145,115 @@ def tile_list_competition_dispersal_kernel(
                 in_=ws_bf[a][:].rearrange("p c i -> p (c i)"),
             )
 
-        wd_codes = keep.tile([P, GROUPS, 512], U32, name="wd_codes", align_bytes=64)
-        wd_planes = keep.tile([P, GROUPS, 512], U8, align_bytes=64)
+        wd_codes = keep.tile([P, GROUPS, PASS_ROWS], U32, name="wd_codes", align_bytes=64)
+        wd_planes = keep.tile([P, GROUPS, PASS_ROWS], U8, align_bytes=64)
 
-        def quantise_wd(g, t0, t1, tag):
-            grouped = keep.tile([P, t1 - t0, P, 4], BF16, name="wd_bf", tag=tag, align_bytes=64)
+        def quantise_wd(g, tag):
+            grouped = keep.tile([P, 4, P, 4], BF16, name="wd_bf", tag=tag, align_bytes=64)
             nc.scalar.copy(out=grouped[:].rearrange("p t m i -> p m i t"),
-                           in_=wd_raw[g][:].rearrange("p i (m t) -> p m i t", t=4)[:, :, :, t0:t1])
-            cols = slice(t0 * P, t1 * P)
+                           in_=wd_raw[g][:].rearrange("p i (m t) -> p m i t", t=4))
             nc.vector.quantize_mx(
-                out=wd_codes[:, g, cols].bitcast(FP8X4), scales=wd_planes[:, g, cols],
+                out=wd_codes[:, g, :].bitcast(FP8X4), scales=wd_planes[:, g, :],
                 in_=grouped[:].rearrange("p t m i -> p (t m i)"),
             )
 
-        def stationary(lst, a, blk):
+        free_banks = list(range(BANKS))
+
+        def take_bank(shape, name):
+            number = free_banks[0]
+            free_banks.remove(number)
+            return psum.tile(shape, F32, name=name, tag="bank%d" % number), number
+
+        def multiply(bank, lst, a, blk, words, plane, start, stop):
             half, c0 = divmod(blk * BLOCK, HALF)
-            cols = slice(blk * BLOCK, (blk + 1) * BLOCK)
-            words = picked[lst, a, half][:, c0 : c0 + BLOCK].bitcast(FP8X4)
-            plane = (planes, lifted)[a][:, lst, cols]
-            return words, plane
+            nc.tensor.matmul_mx(
+                out=bank[:],
+                lhsT=picked[lst, a, half][:, c0 : c0 + BLOCK].bitcast(FP8X4),
+                lhsT_scale=(planes, lifted)[a][:, lst, blk * BLOCK : (blk + 1) * BLOCK],
+                rhs=words, rhs_scale=plane, start=start, stop=stop,
+            )
 
-        def product(bank, terms, blk, start=True, stop=True):
-            for n, (lst, a, words, plane) in enumerate(terms):
-                lhs, lhs_plane = stationary(lst, a, blk)
-                nc.tensor.matmul_mx(out=bank[:], lhsT=lhs, lhsT_scale=lhs_plane, rhs=words, rhs_scale=plane,
-                                    start=(start and n == 0), stop=(stop and n == len(terms) - 1))
-
-        room, c_banks = {}, {}
-
-        def new_bank(shape, name, b):
-            return psum.tile(shape, F32, name=name, tag="bank%d" % b)
+        crowd, abund, pred, room = {}, {}, {}, {}
 
         def crowding(blk, lst, a):
-            first, last = (lst, a) == (1, 0), (lst, a) == (0, 1)
+            first, last = (lst, a) == (COMPETITOR, 0), (lst, a) == (SPECIES, PASSES - 1)
             if first:
-                c_banks[blk] = new_bank([P, H], "crowd_bank", blk)
-            if lst == 1:
-                term = (1, a, wc[:, a, :].bitcast(FP4X4), w_planes[:, 1, a, :])
-            else:
-                term = (0, a, wi[a][:].bitcast(FP8X4), w_planes[:, 0, a, :])
-            product(c_banks[blk], [term], blk, start=first, stop=last)
+                crowd[blk] = take_bank([P, H], "crowd_bank")
+            words = wc[:, a, :].bitcast(FP4X4) if lst == COMPETITOR else wi[a][:].bitcast(FP8X4)
+            multiply(crowd[blk][0], lst, a, blk, words, w_planes[:, lst, a, :], first, last)
 
-        def by_word(rows):
-            return rows.rearrange("j (p u e) -> j u p e", u=2, e=2)
+        def abundance(blk):
+            abund[blk] = take_bank([P, H], "a_bank")
+            for a in range(PASSES):
+                multiply(abund[blk][0], SPECIES, a, blk, ws_codes[:, a, :].bitcast(FP8X4), ws_planes[:, a, :],
+                         a == 0, a == PASSES - 1)
 
-        def as_words(rows):
+        def predation(blk):
+            pred[blk] = take_bank([P, H], "p_bank")
+            for a in range(PASSES):
+                multiply(pred[blk][0], PREDATOR, a, blk, wp[:, a, :].bitcast(FP4X4), w_planes[:, PREDATOR, a, :],
+                         a == 0, a == PASSES - 1)
+
+        def bank_walk(bank):
+            return bank[:].rearrange("j (p u e) -> j u p e", u=2, e=2)
+
+        def rows_walk(rows):
             return rows.rearrange("j (u p e) -> j u p e", u=2, e=2)
 
         def make_rooms():
-            later = keep.tile([P, 6, H], F32, name="rooms", tag="ws_raw0", align_bytes=64)
-            for blk in range(8):
+            later = keep.tile([P, BLOCKS - 2, H], F32, name="rooms", tag="ws_raw0", align_bytes=64)
+            for blk in range(BLOCKS):
                 if blk < 2:
                     room[blk] = keep.tile([P, H], F32, name="room%d" % blk, align_bytes=64)[:]
                 else:
                     room[blk] = later[:, blk - 2, :]
-                nc.scalar.activation(out=as_words(room[blk]), in_=by_word(c_banks[blk][:]), func=COPY, scale=-1.0, bias=1.0)
+                nc.scalar.activation(out=rows_walk(room[blk]), in_=bank_walk(crowd[blk][0]),
+                                     func=COPY, scale=-1.0, bias=1.0)
+                free_banks.append(crowd[blk][1])
 
-        h_quant, h_rows = {}, {}
-
-        a_banks, p_banks = {}, {}
-
-        def abundance(blk, b):
-            a_banks[blk] = new_bank([P, H], "a_bank", b)
-            product(a_banks[blk], [(0, a, ws_codes[:, a, :].bitcast(FP8X4), ws_planes[:, a, :]) for a in range(PASSES)], blk)
-
-        def predation(blk, b):
-            p_banks[blk] = new_bank([P, H], "p_bank", b)
-            product(p_banks[blk], [(2, a, wp[:, a, :].bitcast(FP4X4), w_planes[:, 2, a, :]) for a in range(PASSES)], blk)
+        h_rows, h_grouped, h_codes = {}, {}, {}
 
         def growth(quarter):
             blks = (2 * quarter, 2 * quarter + 1)
-            grown, hs = {}, {}
+            grown = {}
             for blk in blks:
                 grown[blk] = ring.tile([P, H], F32, name="grown", tag="grown")
-                nc.vector.tensor_tensor(as_words(grown[blk][:]), by_word(a_banks[blk][:]), as_words(room[blk]), MULT)
-            both = keep.tile([P, 2, H], BF16, name="h_rows", tag="h%d" % quarter, align_bytes=64)
-            for blk in blks:
-                hs[blk] = both[:, blk % 2, :]
-                nc.vector.tensor_tensor(as_words(hs[blk]), as_words(grown[blk][:]), by_word(p_banks[blk][:]), SUBTRACT)
-            h_rows[quarter] = hs
-
-        def turn(quarter, bank_no):
-            blks = (2 * quarter, 2 * quarter + 1)
-            hs = h_rows[quarter]
-            turned = new_bank([P, 2, 2, BLOCK], "turned", bank_no)
+                nc.vector.tensor_tensor(rows_walk(grown[blk][:]), bank_walk(abund[blk][0]), rows_walk(room[blk]), MULT)
+                free_banks.append(abund[blk][1])
+            rows = keep.tile([P, 2, H], BF16, name="h_rows", tag="h%d" % quarter, align_bytes=64)
             for b, blk in enumerate(blks):
-                words = hs[blk].bitcast(F32)
+                nc.vector.tensor_tensor(rows_walk(rows[:, b, :]), rows_walk(grown[blk][:]), bank_walk(pred[blk][0]), SUBTRACT)
+                free_banks.append(pred[blk][1])
+            h_rows[quarter] = rows
+
+        def turn(quarter):
+            turned, number = take_bank([P, 2, 2, BLOCK], "turned")
+            for b in range(2):
+                words = h_rows[quarter][:, b, :].bitcast(F32)
                 for u in range(2):
                     nc.tensor.transpose(turned[:, b, u, :], words[:, u * P : (u + 1) * P], ident[:])
             grouped = keep.tile([P, QUARTER * 4], BF16, name="h_grouped", tag="hg%d" % quarter, align_bytes=64)
             nc.scalar.copy(out=grouped[:].bitcast(F32).rearrange("p (b j u) -> p b j u", b=2, u=2),
                            in_=turned[:].rearrange("p b u j -> p b j u"))
-            h_quant[quarter] = grouped
+            free_banks.append(number)
+            h_grouped[quarter] = grouped
 
         y_planes = keep.tile([P, GROUPS, S], U8, name="y_planes", align_bytes=64)
-        h_codes = {}
 
         def quantise_h(quarter):
-            codes = ring.tile([P, QUARTER], U32, name="h_codes", tag="h_codes", bufs=4, align_bytes=64)
-            plane = ring.tile([P, QUARTER], U8, name="h_plane", tag="h_plane", bufs=4, align_bytes=64)
-            nc.vector.quantize_mx(out=codes[:].bitcast(FP8X4), scales=plane[:], in_=h_quant[quarter][:])
+            codes = ring.tile([P, QUARTER], U32, name="h_codes", tag="h_codes", bufs=QUARTERS, align_bytes=64)
+            plane = ring.tile([P, QUARTER], U8, name="h_plane", tag="h_plane", bufs=QUARTERS, align_bytes=64)
+            nc.vector.quantize_mx(out=codes[:].bitcast(FP8X4), scales=plane[:], in_=h_grouped[quarter][:])
             h_codes[quarter] = (codes, plane)
 
-        def disperse(quarter, g, banks, on_vector=()):
+        ys, y_bf = {}, {}
+
+        def disperse(quarter, g):
             cols = slice(quarter * QUARTER, (quarter + 1) * QUARTER)
             codes, plane = h_codes[quarter]
-            y = ring.tile([P, 4, QUARTER], F32, name="y", tag="y", bufs=8)
+            y = ring.tile([P, 4, QUARTER], F32, name="y", tag="y", bufs=QUARTERS * GROUPS)
             for pair in range(2):
-                bank = new_bank([P, 2, QUARTER], "y_bank", banks[pair])
+                bank, number = take_bank([P, 2, QUARTER], "y_bank")
                 for e in range(2):
                     t = 2 * pair + e
                     nc.tensor.matmul_mx(
@@ -256,112 +262,90 @@ def tile_list_competition_dispersal_kernel(
                         lhsT_scale=wd_planes[:, g, t * P : (t + 1) * P],
                         rhs=codes[:].bitcast(FP8X4), rhs_scale=plane[:], start=True, stop=True,
                     )
-                if pair in on_vector:
-                    ts = slice(2 * pair, 2 * pair + 2)
-                    nc.vector.tensor_tensor(
-                        y[:, ts, :], bank[:], gains[:, g, ts].unsqueeze(2).to_broadcast([P, 2, QUARTER]), MULT)
-                else:
-                    for e in range(2):
-                        t = 2 * pair + e
-                        nc.scalar.activation(out=y[:, t, :], in_=bank[:, e, :], func=COPY, scale=gains[:, g, t : t + 1])
+                for e in range(2):
+                    t = 2 * pair + e
+                    nc.scalar.activation(out=y[:, t, :], in_=bank[:, e, :], func=COPY, scale=gains[:, g, t : t + 1])
+                free_banks.append(number)
             nc.sync.dma_start(
-                out=out_0[512 * g : 512 * (g + 1), cols].rearrange("(p t) j -> p t j", t=4), in_=y[:])
+                out=out_0[PASS_ROWS * g : PASS_ROWS * (g + 1), cols].rearrange("(p t) j -> p t j", t=4), in_=y[:])
             ys[quarter, g] = y
 
-        ys, y_bf = {}, {}
-        y_codes = [keep.tile([P, GROUPS, QUARTER], U32, name="y_codes%d" % q, align_bytes=64) for q in range(4)]
+        y_codes = [keep.tile([P, GROUPS, QUARTER], U32, name="y_codes%d" % q, align_bytes=64) for q in range(QUARTERS)]
 
-        def regroup(quarter, g, cast):
-            y = ys[quarter, g]
-            grouped = ring.tile([P, QUARTER, 4], BF16, name="y_grouped", tag="y_grouped", bufs=8, align_bytes=64)
-            cast(out=grouped[:].rearrange("p (c n) t -> p c t n", n=4), in_=y[:].rearrange("p t (c n) -> p c t n", n=4))
-            y_bf[quarter, g] = grouped
-
-        def quantise_y(quarter, g):
+        def planes_of_y(quarter):
             cols = slice(quarter * QUARTER, (quarter + 1) * QUARTER)
-            nc.vector.quantize_mx(out=y_codes[quarter][:, g, :].bitcast(FP8X4), scales=y_planes[:, g, cols],
-                                  in_=y_bf[quarter, g][:].rearrange("p j t -> p (j t)"))
-
-        def store_codes(quarter):
-            cols = slice(quarter * QUARTER, (quarter + 1) * QUARTER)
-            nc.sync.dma_start(
-                out=out_1[:, :, cols, :].rearrange("g p m t -> p g (m t)").bitcast(I32), in_=y_codes[quarter][:].bitcast(I32))
-
-        def store_scales(cols):
-            for r in range(4):
-                nc.sync.dma_start(
-                    out=out_2[:, r:16:4, cols].rearrange("g q m -> q g m").bitcast(I32),
-                    in_=y_planes[r:P:32, :, cols].bitcast(I32),
-                )
-
-        on_s, on_v = nc.scalar.copy, nc.vector.tensor_copy
-        casts = (on_v, on_v, on_v, on_v, on_v, on_v, on_v, on_v)
-
-        def finish(quarter):
             for g in range(GROUPS):
-                regroup(quarter, g, casts[2 * quarter + g])
+                grouped = ring.tile([P, QUARTER, 4], BF16, name="y_grouped", tag="y_grouped",
+                                    bufs=QUARTERS * GROUPS, align_bytes=64)
+                nc.vector.tensor_copy(out=grouped[:].rearrange("p (c n) t -> p c t n", n=4),
+                                      in_=ys[quarter, g][:].rearrange("p t (c n) -> p c t n", n=4))
+                y_bf[quarter, g] = grouped
             for g in range(GROUPS):
-                quantise_y(quarter, g)
-            store_codes(quarter)
+                nc.vector.quantize_mx(out=y_codes[quarter][:, g, :].bitcast(FP8X4), scales=y_planes[:, g, cols],
+                                      in_=y_bf[quarter, g][:].rearrange("p j t -> p (j t)"))
+            nc.sync.dma_start(out=out_1[:, :, cols, :].rearrange("g p m t -> p g (m t)").bitcast(I32),
+                              in_=y_codes[quarter][:].bitcast(I32))
 
-        for half in range(2):
-            for lst in (1, 0):
-                gather_words(lst, 0, half, "w%d0%d" % (lst, half))
-        gather_words(2, 0, 0, "w200")
-        for half in range(2):
-            for lst in (1, 0):
-                gather_words(lst, 1, half, "w%d1%d" % (lst, half))
-        gather_words(2, 1, 0, "w210")
-        round_ws(0, on_s)
-        round_ws(1, on_v)
+        def crowd_gathers(a):
+            for half in range(2):
+                for lst in (COMPETITOR, SPECIES):
+                    gather_words(lst, a, half, "w%d%d%d" % (lst, a, half))
+
+        crowd_gathers(0)
+        gather_words(PREDATOR, 0, 0, "w200")
+        crowd_gathers(1)
+        gather_words(PREDATOR, 1, 0, "w210")
+        round_ws(0, nc.scalar.copy)
+        round_ws(1, nc.vector.tensor_copy)
         quantise_ws(0)
         quantise_ws(1)
-        gather_words(2, 0, 1, "ws_bf1")
+        gather_words(PREDATOR, 0, 1, "ws_bf1")
         for a in range(PASSES):
             for half in range(2):
-                for lst in (1, 0):
+                for lst in (COMPETITOR, SPECIES):
                     for blk in range(4 * half, 4 * half + 4):
                         crowding(blk, lst, a)
         make_rooms()
-        predation(0, 0)
-        predation(1, 1)
+        predation(0)
+        predation(1)
         for blk in range(4):
-            abundance(blk, 2 + blk)
-        predation(2, 6)
-        predation(3, 7)
-        quantise_wd(0, 0, 4, "wd0")
+            abundance(blk)
+        predation(2)
+        predation(3)
+        quantise_wd(0, "wd0")
         growth(0)
-        gather_words(2, 1, 1, "room1")
-        turn(0, 2)
+        gather_words(PREDATOR, 1, 1, "room1")
+        turn(0)
         quantise_h(0)
-        quantise_wd(1, 0, 4, "h0")
-        abundance(4, 3)
-        abundance(5, 0)
+        quantise_wd(1, "h0")
+        abundance(4)
+        abundance(5)
         growth(1)
-        disperse(0, 0, (1, 2))
-        turn(1, 4)
+        disperse(0, 0)
+        turn(1)
         quantise_h(1)
-        predation(4, 5)
-        predation(5, 6)
-        disperse(0, 1, (7, 1))
+        predation(4)
+        predation(5)
+        disperse(0, 1)
         growth(2)
-        abundance(6, 4)
-        abundance(7, 3)
-        disperse(1, 0, (2, 7))
-        predation(6, 0)
-        predation(7, 5)
-        turn(2, 6)
+        abundance(6)
+        abundance(7)
+        disperse(1, 0)
+        predation(6)
+        predation(7)
+        turn(2)
         quantise_h(2)
-        disperse(1, 1, (1, 2))
+        disperse(1, 1)
         growth(3)
-        turn(3, 7)
+        turn(3)
         quantise_h(3)
-        disperse(2, 0, (6, 1))
-        disperse(2, 1, (2, 4))
-        disperse(3, 0, (3, 0))
-        disperse(3, 1, (5, 7))
-        finish(0)
-        finish(1)
-        finish(2)
-        finish(3)
-        store_scales(slice(0, S))
+        for quarter in (2, 3):
+            for g in range(GROUPS):
+                disperse(quarter, g)
+        for quarter in range(QUARTERS):
+            planes_of_y(quarter)
+        for r in range(4):
+            nc.sync.dma_start(
+                out=out_2[:, r:16:4, :].rearrange("g q m -> q g m").bitcast(I32),
+                in_=y_planes[r:P:32, :, :].bitcast(I32),
+            )

@@ -223,11 +223,12 @@ def tile_list_competition_dispersal_kernel(
             rows = keep.tile([P, 2, H], BF16, name="h_rows", tag="h%d" % quarter, align_bytes=64)
             for b, blk in enumerate(blks):
                 nc.vector.tensor_tensor(rows_walk(rows[:, b, :]), rows_walk(grown[blk][:]), bank_walk(pred[blk][0]), SUBTRACT)
-                free_banks.append(pred[blk][1])
+            free_banks.append(pred[blks[0]][1])
             h_rows[quarter] = rows
 
         def turn(quarter):
-            turned, number = take_bank([P, 2, 2, BLOCK], "turned")
+            number = pred[2 * quarter + 1][1]
+            turned = psum.tile([P, 2, 2, BLOCK], F32, name="turned", tag="bank%d" % number)
             for b in range(2):
                 words = h_rows[quarter][:, b, :].bitcast(F32)
                 for u in range(2):

@@ -113,9 +113,9 @@ def tile_list_competition_dispersal_kernel(
         load_ws(1)
         wp = load_fp4("wp", wp_words)
         load_wd(0)
+        load_wd(1)
         gains = keep.tile([P, GROUPS, 4], F32, name="gains")
         nc.sync.dma_start(out=gains[:], in_=gain.rearrange("(g p t) -> p g t", g=GROUPS, t=4))
-        load_wd(1)
 
         ident = keep.tile([P, P], F32, name="ident")
         nc.vector.memset(ident[:], 0.0)

from contextlib import ExitStack

import concourse.mybir as mybir
from concourse.masks import make_identity

K, T, S, H, N = 1024, 4096, 1024, 512, 1024
FLOPS = 2 * (4 * K * H * S + H * N * S)

F32 = mybir.dt.float32
BF16 = mybir.dt.bfloat16
I32 = mybir.dt.int32
U32 = mybir.dt.uint32
U16 = mybir.dt.uint16
U8 = mybir.dt.uint8
FP8X4 = mybir.dt.float8_e4m3fn_x4
FP4X4 = mybir.dt.float4_e2m1fn_x4
COPY = mybir.ActivationFunctionType.Copy
MULT = mybir.AluOpType.mult
SUBTRACT = mybir.AluOpType.subtract

P = 128
PASS_ROWS = 512
PASSES = K // PASS_ROWS
GROUPS = N // PASS_ROWS
HALF = 512
QUARTER = 256
BLOCK = 128
BLOCKS = S // BLOCK
QUARTERS = S // QUARTER
BANKS = 8
PER_COLUMN = 16
SECOND_PASS = 16
SPECIES, COMPETITOR, PREDATOR = 0, 1, 2


def tile_list_competition_dispersal_kernel(
    tc, tab_words, tab_scales, offs, offs2, offs3, ws, wi_words, wi_scales,
    wc_words, wc_scales, wp_words, wp_scales, wd, gain, out_0, out_1, out_2,
):
    nc = tc.nc
    with ExitStack() as ctx:
        keep = ctx.enter_context(tc.tile_pool(name="keep", bufs=1))
        ring = ctx.enter_context(tc.tile_pool(name="ring", bufs=2))
        psum = ctx.enter_context(tc.psum_pool(name="psum", bufs=1))

        tab_plane = keep.tile([P, T], U8, name="tab_plane", align_bytes=64)
        nc.vector.memset(tab_plane[:].bitcast(I32), 0)
        lists = [keep.tile([P, S // PER_COLUMN], U16, name="list%d" % n) for n in range(3)]
        nc.sync.dma_start(lists[COMPETITOR][:], offs2)
        staged = keep.tile([16, 3, PASSES, H], U8, name="staged", align_bytes=64)
        for w, src in enumerate((wi_scales, wc_scales, wp_scales)):
            nc.sync.dma_start(out=staged[:, w, :, :].bitcast(I32), in_=src.rearrange("a q c -> q a c").bitcast(I32))
        for r in range(4):
            nc.sync.dma_start(
                out=tab_plane[r:P:SECOND_PASS, :].bitcast(I32),
                in_=tab_scales.rearrange("a (q r) t -> r q a t", r=4)[r].bitcast(I32),
            )
        nc.sync.dma_start(lists[SPECIES][:], offs)
        nc.sync.dma_start(lists[PREDATOR][:], offs3)

        tab, wi, ws_raw, wd_raw = [], [], [], []

        def load_table(a):
            words = keep.tile([P, T], I32, name="tab%d" % a, align_bytes=64)
            nc.sync.dma_start(out=words[:], in_=tab_words[a].rearrange("p t i -> p (t i)").bitcast(I32))
            tab.append(words)

        def load_wi(a):
            words = keep.tile([P, H], I32, name="wi%d" % a, align_bytes=64)
            nc.sync.dma_start(out=words[:], in_=wi_words[a].rearrange("p c i -> p (c i)").bitcast(I32))
            wi.append(words)

        def load_fp4(name, src):
            words = keep.tile([P, PASSES, 2 * H], U8, name=name, align_bytes=64)
            nc.sync.dma_start(out=words[:].bitcast(I32), in_=src.rearrange("a p c -> p a c").bitcast(I32))
            return words

        def load_ws(a):
            raw = keep.tile([P, 4, H], F32, name="ws_raw%d" % a, tag="ws_raw%d" % a, align_bytes=64)
            rows = ws[PASS_ROWS * a : PASS_ROWS * (a + 1), :]
            nc.sync.dma_start(out=raw[:], in_=rows.rearrange("(p i) c -> p i c", i=4))
            ws_raw.append(raw)

        def load_wd(g):
            raw = keep.tile([P, 4, PASS_ROWS], F32, name="wd_raw%d" % g)
            cols = wd[:, PASS_ROWS * g : PASS_ROWS * (g + 1)]
            nc.sync.dma_start(out=raw[:], in_=cols.rearrange("(p i) n -> p i n", i=4))
            wd_raw.append(raw)

        load_table(0)
        wc = load_fp4("wc", wc_words)
        load_wi(0)
        w_planes = keep.tile([P, 3, PASSES, H], U8, name="w_planes", align_bytes=64)
        flat_planes = w_planes[:].rearrange("p w a c -> p (w a c)").bitcast(I32)
        flat_staged = staged[:].rearrange("p w a c -> p (w a c)").bitcast(I32)
        nc.vector.memset(flat_planes, 0)
        for r in range(4):
            nc.sync.dma_start(out=flat_planes[r:P:32, :], in_=flat_staged[r:16:4, :])
        load_table(1)

        planes = keep.tile([P, 3, S], U8, name="planes", align_bytes=64)
        for lst in (COMPETITOR, SPECIES, PREDATOR):
            nc.vector.tensor_copy(planes[:, lst, :], tab_plane[:].indirect(lists[lst][:]))
        lifted = keep.tile([P, 3, S], U8, name="lifted", align_bytes=64)
        nc.vector.memset(lifted[:].rearrange("p l s -> p (l s)").bitcast(I32), 0)
        nc.sync.dma_start(
            out=lifted[0 : P - SECOND_PASS].rearrange("p l s -> p (l s)").bitcast(I32),
            in_=planes[SECOND_PASS:P].rearrange("p l s -> p (l s)").bitcast(I32),
        )

        load_wi(1)
        load_ws(0)
        load_ws(1)
        wp = load_fp4("wp", wp_words)
        load_wd(0)
        load_wd(1)
        gains = keep.tile([P, GROUPS, 4], F32, name="gains")
        nc.sync.dma_start(out=gains[:], in_=gain.rearrange("(g p t) -> p g t", g=GROUPS, t=4))

        ident = keep.tile([P, P], F32, name="ident")
        nc.vector.memset(ident[:], 0.0)
        make_identity(nc, ident[:], nomemset=True)

        picked = {}

        def gather_words(lst, a, half, tag):
            words = keep.tile([P, HALF], U32, name="picked_%d_%d_%d" % (lst, a, half), tag=tag, align_bytes=64)
            cols = slice(half * HALF // PER_COLUMN, (half + 1) * HALF // PER_COLUMN)
            nc.vector.tensor_copy(words[:], tab[a][:].bitcast(U32).indirect(lists[lst][:, cols]))
            picked[lst, a, half] = words[:]

        ws_codes = keep.tile([P, PASSES, H], U32, name="ws_codes", align_bytes=64)
        ws_planes = keep.tile([P, PASSES, H], U8, align_bytes=64)
        ws_bf = {}

        def round_ws(a, copy):
            grouped = keep.tile([P, H, 4], BF16, name="ws_bf%d" % a, tag="ws_bf%d" % a, align_bytes=64)
            copy(out=grouped[:].rearrange("p (c n) i -> p c i n", n=4),
                 in_=ws_raw[a][:].rearrange("p i (c n) -> p c i n", n=4))
            ws_bf[a] = grouped

        def quantise_ws(a):
            nc.vector.quantize_mx(
                out=ws_codes[:, a, :].bitcast(FP8X4), scales=ws_planes[:, a, :],
                in_=ws_bf[a][:].rearrange("p c i -> p (c i)"),
            )

        wd_codes = keep.tile([P, GROUPS, PASS_ROWS], U32, name="wd_codes", align_bytes=64)
        wd_planes = keep.tile([P, GROUPS, PASS_ROWS], U8, align_bytes=64)

        def quantise_wd(g, tag):
            grouped = keep.tile([P, 4, P, 4], BF16, name="wd_bf", tag=tag, align_bytes=64)
            nc.scalar.copy(out=grouped[:].rearrange("p t m i -> p m i t"),
                           in_=wd_raw[g][:].rearrange("p i (m t) -> p m i t", t=4))
            nc.vector.quantize_mx(
                out=wd_codes[:, g, :].bitcast(FP8X4), scales=wd_planes[:, g, :],
                in_=grouped[:].rearrange("p t m i -> p (t m i)"),
            )

        free_banks = list(range(BANKS))

        def take_bank(shape, name):
            number = free_banks[0]
            free_banks.remove(number)
            return psum.tile(shape, F32, name=name, tag="bank%d" % number), number

        def multiply(bank, lst, a, blk, words, plane, start, stop):
            half, c0 = divmod(blk * BLOCK, HALF)
            nc.tensor.matmul_mx(
                out=bank[:],
                lhsT=picked[lst, a, half][:, c0 : c0 + BLOCK].bitcast(FP8X4),
                lhsT_scale=(planes, lifted)[a][:, lst, blk * BLOCK : (blk + 1) * BLOCK],
                rhs=words, rhs_scale=plane, start=start, stop=stop,
            )

        crowd, abund, pred, room = {}, {}, {}, {}

        def crowding(blk, lst, a):
            first, last = (lst, a) == (COMPETITOR, 0), (lst, a) == (SPECIES, PASSES - 1)
            if first:
                crowd[blk] = take_bank([P, H], "crowd_bank")
            words = wc[:, a, :].bitcast(FP4X4) if lst == COMPETITOR else wi[a][:].bitcast(FP8X4)
            multiply(crowd[blk][0], lst, a, blk, words, w_planes[:, lst, a, :], first, last)

        def abundance(blk):
            abund[blk] = take_bank([P, H], "a_bank")
            for a in range(PASSES):
                multiply(abund[blk][0], SPECIES, a, blk, ws_codes[:, a, :].bitcast(FP8X4), ws_planes[:, a, :],
                         a == 0, a == PASSES - 1)

        def predation(blk):
            pred[blk] = take_bank([P, H], "p_bank")
            for a in range(PASSES):
                multiply(pred[blk][0], PREDATOR, a, blk, wp[:, a, :].bitcast(FP4X4), w_planes[:, PREDATOR, a, :],
                         a == 0, a == PASSES - 1)

        def bank_walk(bank):
            return bank[:].rearrange("j (p u e) -> j u p e", u=2, e=2)

        def rows_walk(rows):
            return rows.rearrange("j (u p e) -> j u p e", u=2, e=2)

        def make_rooms():
            later = keep.tile([P, BLOCKS - 2, H], F32, name="rooms", tag="ws_raw0", align_bytes=64)
            for blk in range(BLOCKS):
                if blk < 2:
                    room[blk] = keep.tile([P, H], F32, name="room%d" % blk, align_bytes=64)[:]
                else:
                    room[blk] = later[:, blk - 2, :]
                nc.scalar.activation(out=rows_walk(room[blk]), in_=bank_walk(crowd[blk][0]),
                                     func=COPY, scale=-1.0, bias=1.0)
                free_banks.append(crowd[blk][1])

        h_rows, h_grouped, h_codes = {}, {}, {}

        def growth(quarter):
            blks = (2 * quarter, 2 * quarter + 1)
            grown = {}
            for blk in blks:
                grown[blk] = ring.tile([P, H], F32, name="grown", tag="grown")
                nc.vector.tensor_tensor(rows_walk(grown[blk][:]), bank_walk(abund[blk][0]), rows_walk(room[blk]), MULT)
                free_banks.append(abund[blk][1])
            rows = keep.tile([P, 2, H], BF16, name="h_rows", tag="h%d" % quarter, align_bytes=64)
            for b, blk in enumerate(blks):
                nc.vector.tensor_tensor(rows_walk(rows[:, b, :]), rows_walk(grown[blk][:]), bank_walk(pred[blk][0]), SUBTRACT)
            free_banks.append(pred[blks[0]][1])
            h_rows[quarter] = rows

        def turn(quarter):
            number = pred[2 * quarter + 1][1]
            turned = psum.tile([P, 2, 2, BLOCK], F32, name="turned", tag="bank%d" % number)
            for b in range(2):
                words = h_rows[quarter][:, b, :].bitcast(F32)
                for u in range(2):
                    nc.tensor.transpose(turned[:, b, u, :], words[:, u * P : (u + 1) * P], ident[:])
            grouped = keep.tile([P, QUARTER * 4], BF16, name="h_grouped", tag="hg%d" % quarter, align_bytes=64)
            nc.scalar.copy(out=grouped[:].bitcast(F32).rearrange("p (b j u) -> p b j u", b=2, u=2),
                           in_=turned[:].rearrange("p b u j -> p b j u"))
            free_banks.append(number)
            h_grouped[quarter] = grouped

        y_planes = keep.tile([P, GROUPS, S], U8, name="y_planes", align_bytes=64)

        def quantise_h(quarter):
            codes = ring.tile([P, QUARTER], U32, name="h_codes", tag="h_codes", bufs=QUARTERS, align_bytes=64)
            plane = ring.tile([P, QUARTER], U8, name="h_plane", tag="h_plane", bufs=QUARTERS, align_bytes=64)
            nc.vector.quantize_mx(out=codes[:].bitcast(FP8X4), scales=plane[:], in_=h_grouped[quarter][:])
            h_codes[quarter] = (codes, plane)

        ys, y_bf = {}, {}

        def disperse(quarter, g):
            cols = slice(quarter * QUARTER, (quarter + 1) * QUARTER)
            codes, plane = h_codes[quarter]
            y = ring.tile([P, 4, QUARTER], F32, name="y", tag="y", bufs=QUARTERS * GROUPS)
            for pair in range(2):
                bank, number = take_bank([P, 2, QUARTER], "y_bank")
                for e in range(2):
                    t = 2 * pair + e
                    nc.tensor.matmul_mx(
                        out=bank[:, e, :],
                        lhsT=wd_codes[:, g, t * P : (t + 1) * P].bitcast(FP8X4),
                        lhsT_scale=wd_planes[:, g, t * P : (t + 1) * P],
                        rhs=codes[:].bitcast(FP8X4), rhs_scale=plane[:], start=True, stop=True,
                    )
                for e in range(2):
                    t = 2 * pair + e
                    nc.scalar.activation(out=y[:, t, :], in_=bank[:, e, :], func=COPY, scale=gains[:, g, t : t + 1])
                free_banks.append(number)
            nc.sync.dma_start(
                out=out_0[PASS_ROWS * g : PASS_ROWS * (g + 1), cols].rearrange("(p t) j -> p t j", t=4), in_=y[:])
            ys[quarter, g] = y

        y_codes = [keep.tile([P, GROUPS, QUARTER], U32, name="y_codes%d" % q, align_bytes=64) for q in range(QUARTERS)]

        def planes_of_y(quarter):
            cols = slice(quarter * QUARTER, (quarter + 1) * QUARTER)
            for g in range(GROUPS):
                grouped = ring.tile([P, QUARTER, 4], BF16, name="y_grouped", tag="y_grouped",
                                    bufs=QUARTERS * GROUPS, align_bytes=64)
                nc.vector.tensor_copy(out=grouped[:].rearrange("p (c n) t -> p c t n", n=4),
                                      in_=ys[quarter, g][:].rearrange("p t (c n) -> p c t n", n=4))
                y_bf[quarter, g] = grouped
            for g in range(GROUPS):
                nc.vector.quantize_mx(out=y_codes[quarter][:, g, :].bitcast(FP8X4), scales=y_planes[:, g, cols],
                                      in_=y_bf[quarter, g][:].rearrange("p j t -> p (j t)"))
            nc.sync.dma_start(out=out_1[:, :, cols, :].rearrange("g p m t -> p g (m t)").bitcast(I32),
                              in_=y_codes[quarter][:].bitcast(I32))

        def crowd_gathers(a):
            for half in range(2):
                for lst in (COMPETITOR, SPECIES):
                    gather_words(lst, a, half, "w%d%d%d" % (lst, a, half))

        crowd_gathers(0)
        gather_words(PREDATOR, 0, 0, "w200")
        crowd_gathers(1)
        gather_words(PREDATOR, 1, 0, "w210")
        round_ws(0, nc.scalar.copy)
        round_ws(1, nc.vector.tensor_copy)
        quantise_ws(0)
        quantise_ws(1)
        gather_words(PREDATOR, 0, 1, "ws_bf1")
        for a in range(PASSES):
            for half in range(2):
                for lst in (COMPETITOR, SPECIES):
                    for blk in range(4 * half, 4 * half + 4):
                        crowding(blk, lst, a)
        make_rooms()
        predation(0)
        predation(1)
        for blk in range(4):
            abundance(blk)
        predation(2)
        predation(3)
        quantise_wd(0, "wd0")
        growth(0)
        gather_words(PREDATOR, 1, 1, "room1")
        turn(0)
        quantise_h(0)
        quantise_wd(1, "h0")
        abundance(4)
        abundance(5)
        growth(1)
        disperse(0, 0)
        turn(1)
        quantise_h(1)
        predation(4)
        predation(5)
        disperse(0, 1)
        growth(2)
        abundance(6)
        abundance(7)
        disperse(1, 0)
        predation(6)
        predation(7)
        turn(2)
        quantise_h(2)
        disperse(1, 1)
        growth(3)
        turn(3)
        quantise_h(3)
        for quarter in (2, 3):
            for g in range(GROUPS):
                disperse(quarter, g)
        for quarter in range(QUARTERS):
            planes_of_y(quarter)
        for r in range(4):
            nc.sync.dma_start(
                out=out_2[:, r:16:4, :].rearrange("g q m -> q g m").bitcast(I32),
                in_=y_planes[r:P:32, :, :].bitcast(I32),
            )
